import numpy as np
import ml_dtypes


def mxq(x, axis, fmt="e4m3"):
    dtype, down = {"e4m3": (ml_dtypes.float8_e4m3fn, 7), "e5m2": (ml_dtypes.float8_e5m2, 14)}[fmt]
    v = np.moveaxis(np.asarray(x, np.float32).astype(ml_dtypes.bfloat16).astype(np.float64), axis, -1)
    blocks = v.reshape(v.shape[:-1] + (-1, 32))
    amax = np.abs(blocks).max(-1, keepdims=True)
    byte = np.maximum(np.where(amax > 0, np.frexp(amax)[1] - 1 + 127, 0) - down, 1)
    scale = np.exp2(byte - 127.0)
    codes = (blocks / scale).astype(np.float32).astype(dtype).astype(np.float64)
    return np.moveaxis((codes * scale).reshape(v.shape), -1, axis)


WIDE = False


def mx_kscale(k):
    if not WIDE:
        return np.ones(k)
    levels = np.array([10, -10, 5, -5, 0])
    if k % 512:
        return np.exp2(np.random.permutation(np.resize(levels, k // 32))).repeat(32)
    a = np.empty((k // 512, 16))
    for p in range(k // 512):
        a[p, :8] = np.random.permutation(np.resize(levels, 8))
        for g in range(8):
            far = levels[np.abs(levels - a[p, g]) >= 10]
            a[p, g + 8] = far[np.random.randint(len(far))]
    return np.exp2(a.ravel()).repeat(32)


def f64(x):
    return np.asarray(x).astype(np.float64)


def striped(idx):
    return np.tile(idx.reshape(-1, 16).T, (8, 1)).astype(np.uint16)


def unstriped(offs):
    return offs[:16].T.reshape(-1).astype(np.int64)


def pack_weight(w):
    k, n = w.shape
    w = f64(np.asarray(w, np.float32).astype(ml_dtypes.bfloat16)).reshape(k // 32, 32, n)
    amax = np.abs(w).max(1)
    byte = np.clip(np.where(amax > 0, np.frexp(amax)[1] - 1 + 127 - 7, 1), 1, 254)
    scaled = (w * np.exp2(127.0 - byte)[:, None, :]).reshape(k, n).astype(np.float32)
    words = np.ascontiguousarray(scaled.reshape(k // 512, 128, 4, n).transpose(0, 1, 3, 2)).astype(ml_dtypes.float8_e4m3fn).view(np.uint8)
    return words, np.ascontiguousarray(byte.astype(np.uint8).reshape(k // 512, 16, n))


def unpack_weight(words, scales):
    g, p, n, _ = words.shape
    vals = np.ascontiguousarray(words).view(ml_dtypes.float8_e4m3fn).astype(np.float64) * np.repeat(np.exp2(scales.astype(np.float64) - 127.0), 8, axis=1)[..., None]
    return vals.transpose(0, 1, 3, 2).reshape(g * 512, n)


def silu(v):
    return v / (1.0 + np.exp(-np.maximum(v, -700.0)))


K, T, S, D, H, N, U = 512, 2048, 512, 8, 512, 128, 512
P = 2 ** 7


def setup_inputs():
    n = np.random.standard_normal
    s = mx_kscale(K)[:, None]
    u = mx_kscale(H)
    packed_xT = pack_weight(n((K, T)) * s)
    return {
        "x_words": packed_xT[0],
        "x_scales": packed_xT[1],
        "w1": (n((K, H)) / np.sqrt(K) / s * u).astype(np.float32),
        "w2": (n((H, N)) / np.sqrt(H) / u[:, None]).astype(np.float32),
        "total": (np.tile(0.5 * n(S), (P, 1))).astype(np.float32),
        "inv": (np.tile(np.random.uniform(0.1, 1.0, U), (P, 1))).astype(np.float32),
        "offs": striped(np.random.permutation(T)[:S]),
        "pa": striped(np.random.permutation(S)),
        "pb": striped(np.random.permutation(S)),
    }


def reference(x_words, x_scales, w1, w2, total, inv, offs, pa, pb):
    xq = unpack_weight(x_words, x_scales)[:, unstriped(offs)]
    h = silu(mxq(f64(w1), 0, "e4m3").T @ xq)
    y = mxq(f64(w2), 0, "e4m3").T @ mxq(h, 0, "e4m3")
    mq = y.reshape(len(y), -1, D).mean(axis=2)
    ch = y - np.repeat(mq, D, axis=1) + f64(total)[:1]
    pr = ch[:, unstriped(pa)] * ch[:, unstriped(pb)]
    return np.tanh(pr * f64(inv)[:1])

@@ -1,0 +1,165 @@
+from contextlib import ExitStack
+
+import concourse.mybir as mybir
+
+K, T, S, D, H, N, U = 512, 2048, 512, 8, 512, 128, 512
+FLOPS = 2 * K * H * S + 2 * H * N * S
+
+F32 = mybir.dt.float32
+BF16 = mybir.dt.bfloat16
+I32 = mybir.dt.int32
+U32 = mybir.dt.uint32
+U16 = mybir.dt.uint16
+U8 = mybir.dt.uint8
+FP8X4 = mybir.dt.float8_e4m3fn_x4
+ACT = mybir.ActivationFunctionType
+ALU = mybir.AluOpType
+
+P = 128
+PACK = 4
+LIST_ROWS = 16
+CHUNK = 128
+HALF = 256
+
+
+def tile_picked_yqeq_pair_p_kernel(tc, x_words, x_scales, w1, w2, total, inv, offs, pa, pb, out):
+    nc = tc.nc
+    with ExitStack() as ctx:
+        sb = ctx.enter_context(tc.tile_pool(name="sb", bufs=1))
+        ps = ctx.enter_context(tc.psum_pool(name="ps", bufs=1))
+
+        offs_sb = sb.tile([P, S // LIST_ROWS], U16, name="offs_sb")
+        pa_sb = sb.tile([P, U // LIST_ROWS], U16, name="pa_sb")
+        pb_sb = sb.tile([P, U // LIST_ROWS], U16, name="pb_sb")
+        xw = sb.tile([P, T], U32, name="xw", align_bytes=64)
+        xs = sb.tile([P, T], U8, name="xs", align_bytes=64)
+        w1_raw = sb.tile([P, PACK, H], F32, name="w1_raw", align_bytes=64)
+        w2_raw = sb.tile([P, PACK, N], F32, name="w2_raw", align_bytes=64)
+        total_sb = sb.tile([P, S], F32, name="total_sb", align_bytes=64)
+        inv_sb = sb.tile([P, U], F32, name="inv_sb", align_bytes=64)
+
+        nc.vector.memset(xs[:].bitcast(I32), 0)
+        nc.sync.dma_start(offs_sb[:], offs)
+        nc.sync.dma_start(w1_raw[:], w1.rearrange("(p j) c -> p j c", j=PACK))
+        for q in range(4):
+            nc.scalar.dma_start(xs[32 * q : 32 * q + 4, :].bitcast(I32), x_scales[0, 4 * q : 4 * q + 4, :].bitcast(I32))
+        nc.sync.dma_start(xw[:].bitcast(I32), x_words[0].rearrange("p n t -> p (n t)").bitcast(I32))
+        nc.sync.dma_start(w2_raw[:], w2.rearrange("(p j) c -> p j c", j=PACK))
+        nc.sync.dma_start(total_sb[:], total)
+        nc.sync.dma_start(inv_sb[:], inv)
+        nc.sync.dma_start(pa_sb[:], pa)
+        nc.sync.dma_start(pb_sb[:], pb)
+
+        sg = sb.tile([P, S], U8, name="sg", align_bytes=64)
+        nc.vector.tensor_copy(sg[:], xs[:].indirect(offs_sb[:]))
+
+        w1_view = w1_raw[:].rearrange("p j (m t) -> p m j t", t=PACK)
+        w1_codes, w1_scales = [], []
+        w1_bf = []
+        for u in range(2):
+            wb = sb.tile([P, 2, P, PACK], BF16, name="w1_bf%d" % u, align_bytes=64)
+            dst = wb[:].rearrange("p t m j -> p m j t")
+            src = w1_view[:, :, :, 2 * u : 2 * u + 2]
+            if u == 0:
+                nc.vector.tensor_copy(dst, src)
+            else:
+                nc.scalar.activation(dst, src, ACT.Copy)
+            w1_bf.append(wb)
+        for u in range(2):
+            codes = sb.tile([P, 2 * P], U32, name="w1_codes%d" % u, align_bytes=64)
+            scales = sb.tile([P, 2 * P], U8, name="w1_scales%d" % u, align_bytes=64)
+            nc.vector.quantize_mx(out=codes[:].bitcast(FP8X4), scales=scales[:], in_=w1_bf[u][:].rearrange("p t m j -> p (t m j)"))
+            w1_codes.append(codes)
+            w1_scales.append(scales)
+
+        xg = []
+        for u in range(2):
+            g = sb.tile([P, HALF], U32, name="xg%d" % u, align_bytes=64)
+            nc.vector.tensor_copy(g[:], xw[:].indirect(offs_sb[:, 16 * u : 16 * u + 16]))
+            xg.append(g)
+
+        w2_bf = sb.tile([P, N, PACK], BF16, name="w2_bf", align_bytes=64)
+        nc.scalar.activation(
+            w2_bf[:].rearrange("p (c i) j -> p c j i", i=4), w2_raw[:].rearrange("p j (c i) -> p c j i", i=4), ACT.Copy
+        )
+        w2_codes = sb.tile([P, N], U32, name="w2_codes", align_bytes=64)
+        w2_scales = sb.tile([P, N], U8, name="w2_scales", align_bytes=64)
+        nc.vector.quantize_mx(out=w2_codes[:].bitcast(FP8X4), scales=w2_scales[:], in_=w2_bf[:].rearrange("p n j -> p (n j)"))
+
+        nchunks = S // CHUNK
+        ch = sb.tile([P, S], F32, name="ch", align_bytes=64)
+        h_bf, y_ps = [], []
+
+        def layer1(c):
+            hp = ps.tile([P, PACK, CHUNK], F32, name="h_ps%d" % c)
+            u, o = divmod(c * CHUNK, HALF)
+            for t in range(PACK):
+                cols = slice((t % 2) * P, (t % 2 + 1) * P)
+                nc.tensor.matmul_mx(
+                    out=hp[:, t, :],
+                    lhsT=w1_codes[t // 2][:, cols].bitcast(FP8X4),
+                    lhsT_scale=w1_scales[t // 2][:, cols],
+                    rhs=xg[u][:, o : o + CHUNK].bitcast(FP8X4),
+                    rhs_scale=sg[:, c * CHUNK : (c + 1) * CHUNK],
+                    start=True,
+                    stop=True,
+                )
+            hb = sb.tile([P, CHUNK, PACK], BF16, name="h_bf%d" % c, align_bytes=64)
+            nc.scalar.activation(hb[:], hp[:].rearrange("p t n -> p n t"), ACT.Silu)
+            h_bf.append(hb)
+
+        def layer2(c):
+            codes = sb.tile([P, CHUNK], U32, name="h_codes%d" % c, align_bytes=64)
+            scales = sb.tile([P, CHUNK], U8, name="h_scales%d" % c, align_bytes=64)
+            nc.vector.quantize_mx(out=codes[:].bitcast(FP8X4), scales=scales[:], in_=h_bf[c][:].rearrange("p n t -> p (n t)"))
+            yp = ps.tile([P, CHUNK], F32, name="y_ps%d" % c)
+            nc.tensor.matmul_mx(
+                out=yp[:],
+                lhsT=w2_codes[:].bitcast(FP8X4),
+                lhsT_scale=w2_scales[:],
+                rhs=codes[:].bitcast(FP8X4),
+                rhs_scale=scales[:],
+                start=True,
+                stop=True,
+            )
+            y_ps.append(yp)
+
+        def centre(c):
+            cols = slice(c * CHUNK, (c + 1) * CHUNK)
+            mols = CHUNK // D
+            sums = sb.tile([P, mols], F32, name="sums%d" % c)
+            nc.vector.tensor_reduce(sums[:], y_ps[c][:].rearrange("p (v d) -> p v d", d=D), mybir.AxisListType.X, ALU.add)
+            shifted = sb.tile([P, CHUNK], F32, name="shifted%d" % c)
+            nc.vector.tensor_tensor(shifted[:], y_ps[c][:], total_sb[:, cols], ALU.add)
+            nc.vector.scalar_tensor_tensor(
+                ch[:, cols].rearrange("p (v d) -> p v d", d=D),
+                sums[:].unsqueeze(2).to_broadcast([P, mols, D]),
+                -1.0 / D,
+                shifted[:].rearrange("p (v d) -> p v d", d=D),
+                ALU.mult,
+                ALU.add,
+            )
+
+        for c in range(nchunks + 2):
+            if c < nchunks:
+                layer1(c)
+            if 1 <= c <= nchunks:
+                layer2(c - 1)
+            if c >= 2:
+                centre(c - 2)
+
+        left = []
+        for u in range(2):
+            cols = slice(u * HALF, (u + 1) * HALF)
+            a = sb.tile([P, HALF], F32, name="left%d" % u)
+            nc.vector.tensor_tensor(a[:], ch[:].indirect(pa_sb[:, 16 * u : 16 * u + 16]), inv_sb[:, cols], ALU.mult)
+            left.append(a)
+        for lo, hi in ((0, 256), (256, 384), (384, 512)):
+            u, o = divmod(lo, HALF)
+            prod = sb.tile([P, hi - lo], F32, name="prod%d" % lo)
+            nc.vector.tensor_tensor(
+                prod[:], ch[:].indirect(pb_sb[:, lo // LIST_ROWS : hi // LIST_ROWS]), left[u][:, o : o + hi - lo], ALU.mult
+            )
+            res = sb.tile([P, hi - lo], F32, name="res%d" % lo)
+            nc.scalar.activation(res[:], prod[:], ACT.Tanh)
+            nc.sync.dma_start(out[:, lo:hi], res[:])

@@ -39,10 +39,16 @@ def tile_picked_yqeq_pair_p_kernel(tc, x_words, x_scales, w1, w2, total, inv, of
         inv_sb = sb.tile([P, U], F32, name="inv_sb", align_bytes=64)
 
         nc.vector.memset(xs[:].bitcast(I32), 0)
+        warm = sb.tile([P, 1], F32, name="warm")
+        warm_out = sb.tile([P, 1], F32, name="warm_out")
+        nc.gpsimd.memset(warm[:], 0.0)
+        nc.scalar.activation(warm_out[:], warm[:], ACT.Silu)
+        w1_rows = w1.rearrange("(p j) c -> p j c", j=PACK)
+        nc.sync.dma_start(w1_raw[:, 0:2, :], w1_rows[:, 0:2, :])
         nc.sync.dma_start(offs_sb[:], offs)
-        nc.sync.dma_start(w1_raw[:], w1.rearrange("(p j) c -> p j c", j=PACK))
         for q in range(4):
-            nc.scalar.dma_start(xs[32 * q : 32 * q + 4, :].bitcast(I32), x_scales[0, 4 * q : 4 * q + 4, :].bitcast(I32))
+            nc.sync.dma_start(xs[32 * q : 32 * q + 4, :].bitcast(I32), x_scales[0, 4 * q : 4 * q + 4, :].bitcast(I32))
+        nc.sync.dma_start(w1_raw[:, 2:4, :], w1_rows[:, 2:4, :])
         nc.sync.dma_start(xw[:].bitcast(I32), x_words[0].rearrange("p n t -> p (n t)").bitcast(I32))
         nc.sync.dma_start(w2_raw[:], w2.rearrange("(p j) c -> p j c", j=PACK))
         nc.sync.dma_start(total_sb[:], total)
@@ -86,12 +92,13 @@ def tile_picked_yqeq_pair_p_kernel(tc, x_words, x_scales, w1, w2, total, inv, of
         w2_scales = sb.tile([P, N], U8, name="w2_scales", align_bytes=64)
         nc.vector.quantize_mx(out=w2_codes[:].bitcast(FP8X4), scales=w2_scales[:], in_=w2_bf[:].rearrange("p n j -> p (n j)"))
 
-        nchunks = S // CHUNK
+        nbanks = S // CHUNK
+        pieces = [(0, 128), (128, 256), (256, 384), (384, 512)]
         ch = sb.tile([P, S], F32, name="ch", align_bytes=64)
-        h_bf, y_ps = [], []
+        h_ps, h_bf, y_ps, sums, shifted = [], {}, {}, {}, {}
 
         def layer1(c):
-            hp = ps.tile([P, PACK, CHUNK], F32, name="h_ps%d" % c)
+            hp = ps.tile([P, PACK, CHUNK], F32, name="h_ps%d" % c, tag="bank%d" % c)
             u, o = divmod(c * CHUNK, HALF)
             for t in range(PACK):
                 cols = slice((t % 2) * P, (t % 2 + 1) * P)
@@ -104,15 +111,21 @@ def tile_picked_yqeq_pair_p_kernel(tc, x_words, x_scales, w1, w2, total, inv, of
                     start=True,
                     stop=True,
                 )
-            hb = sb.tile([P, CHUNK, PACK], BF16, name="h_bf%d" % c, align_bytes=64)
-            nc.scalar.activation(hb[:], hp[:].rearrange("p t n -> p n t"), ACT.Silu)
-            h_bf.append(hb)
+            h_ps.append(hp)
 
-        def layer2(c):
-            codes = sb.tile([P, CHUNK], U32, name="h_codes%d" % c, align_bytes=64)
-            scales = sb.tile([P, CHUNK], U8, name="h_scales%d" % c, align_bytes=64)
-            nc.vector.quantize_mx(out=codes[:].bitcast(FP8X4), scales=scales[:], in_=h_bf[c][:].rearrange("p n t -> p (n t)"))
-            yp = ps.tile([P, CHUNK], F32, name="y_ps%d" % c)
+        def act(i):
+            lo, hi = pieces[i]
+            c, o = divmod(lo, CHUNK)
+            hb = sb.tile([P, hi - lo, PACK], BF16, name="h_bf%d" % i, align_bytes=64)
+            nc.scalar.activation(hb[:], h_ps[c][:, :, o : o + hi - lo].rearrange("p t n -> p n t"), ACT.Silu)
+            h_bf[i] = hb
+
+        def layer2(i):
+            lo, hi = pieces[i]
+            codes = sb.tile([P, hi - lo], U32, name="h_codes%d" % i, align_bytes=64)
+            scales = sb.tile([P, hi - lo], U8, name="h_scales%d" % i, align_bytes=64)
+            nc.vector.quantize_mx(out=codes[:].bitcast(FP8X4), scales=scales[:], in_=h_bf[i][:].rearrange("p n t -> p (n t)"))
+            yp = ps.tile([P, hi - lo], F32, name="y_ps%d" % i, tag="bank%d" % ((nbanks + i) % 8))
             nc.tensor.matmul_mx(
                 out=yp[:],
                 lhsT=w2_codes[:].bitcast(FP8X4),
@@ -122,31 +135,42 @@ def tile_picked_yqeq_pair_p_kernel(tc, x_words, x_scales, w1, w2, total, inv, of
                 start=True,
                 stop=True,
             )
-            y_ps.append(yp)
+            y_ps[i] = yp
 
-        def centre(c):
-            cols = slice(c * CHUNK, (c + 1) * CHUNK)
-            mols = CHUNK // D
-            sums = sb.tile([P, mols], F32, name="sums%d" % c)
-            nc.vector.tensor_reduce(sums[:], y_ps[c][:].rearrange("p (v d) -> p v d", d=D), mybir.AxisListType.X, ALU.add)
-            shifted = sb.tile([P, CHUNK], F32, name="shifted%d" % c)
-            nc.vector.tensor_tensor(shifted[:], y_ps[c][:], total_sb[:, cols], ALU.add)
+        def read_y(i):
+            lo, hi = pieces[i]
+            sums[i] = sb.tile([P, (hi - lo) // D], F32, name="sums%d" % i)
+            nc.vector.tensor_reduce(sums[i][:], y_ps[i][:].rearrange("p (v d) -> p v d", d=D), mybir.AxisListType.X, ALU.add)
+            shifted[i] = sb.tile([P, hi - lo], F32, name="shifted%d" % i)
+            nc.vector.tensor_tensor(shifted[i][:], y_ps[i][:], total_sb[:, lo:hi], ALU.add)
+
+        def centre(i):
+            lo, hi = pieces[i]
             nc.vector.scalar_tensor_tensor(
-                ch[:, cols].rearrange("p (v d) -> p v d", d=D),
-                sums[:].unsqueeze(2).to_broadcast([P, mols, D]),
+                ch[:, lo:hi].rearrange("p (v d) -> p v d", d=D),
+                sums[i][:].unsqueeze(2).to_broadcast([P, (hi - lo) // D, D]),
                 -1.0 / D,
-                shifted[:].rearrange("p (v d) -> p v d", d=D),
+                shifted[i][:].rearrange("p (v d) -> p v d", d=D),
                 ALU.mult,
                 ALU.add,
             )
 
-        for c in range(nchunks + 2):
-            if c < nchunks:
-                layer1(c)
-            if 1 <= c <= nchunks:
-                layer2(c - 1)
-            if c >= 2:
-                centre(c - 2)
+        for c in range(nbanks):
+            layer1(c)
+        for i in range(len(pieces)):
+            act(i)
+        layer2(0)
+        layer2(1)
+        read_y(0)
+        layer2(2)
+        centre(0)
+        layer2(3)
+        read_y(1)
+        read_y(2)
+        centre(1)
+        read_y(3)
+        centre(2)
+        centre(3)
 
         left = []
         for u in range(2):

@@ -47,7 +47,7 @@ def tile_picked_yqeq_pair_p_kernel(tc, x_words, x_scales, w1, w2, total, inv, of
         nc.sync.dma_start(w1_raw[:, 0:2, :], w1_rows[:, 0:2, :])
         nc.sync.dma_start(offs_sb[:], offs)
         for q in range(4):
-            nc.sync.dma_start(xs[32 * q : 32 * q + 4, :].bitcast(I32), x_scales[0, 4 * q : 4 * q + 4, :].bitcast(I32))
+            nc.sync.dma_start(xs[q:P:32, :].bitcast(I32), x_scales[0, q:16:4, :].bitcast(I32))
         nc.sync.dma_start(w1_raw[:, 2:4, :], w1_rows[:, 2:4, :])
         nc.sync.dma_start(xw[:].bitcast(I32), x_words[0].rearrange("p n t -> p (n t)").bitcast(I32))
         nc.sync.dma_start(w2_raw[:], w2.rearrange("(p j) c -> p j c", j=PACK))
@@ -77,6 +77,18 @@ def tile_picked_yqeq_pair_p_kernel(tc, x_words, x_scales, w1, w2, total, inv, of
             nc.vector.quantize_mx(out=codes[:].bitcast(FP8X4), scales=scales[:], in_=w1_bf[u][:].rearrange("p t m j -> p (t m j)"))
             w1_codes.append(codes)
             w1_scales.append(scales)
+
+        warm_ps = ps.tile([P, 2 * P], F32, name="warm_ps", tag="bank7")
+        for width in (2 * P, 2 * P, P):
+            nc.tensor.matmul_mx(
+                out=warm_ps[:, :width],
+                lhsT=w1_codes[0][:, :P].bitcast(FP8X4),
+                lhsT_scale=w1_scales[0][:, :P],
+                rhs=w1_codes[1][:, :width].bitcast(FP8X4),
+                rhs_scale=w1_scales[1][:, :width],
+                start=True,
+                stop=True,
+            )
 
         xg = []
         for u in range(2):

@@ -60,7 +60,6 @@ def tile_picked_yqeq_pair_p_kernel(tc, x_words, x_scales, w1, w2, total, inv, of
         nc.vector.tensor_copy(sg[:], xs[:].indirect(offs_sb[:]))
 
         w1_view = w1_raw[:].rearrange("p j (m t) -> p m j t", t=PACK)
-        w1_codes, w1_scales = [], []
         w1_bf = []
         for u in range(2):
             wb = sb.tile([P, 2, P, PACK], BF16, name="w1_bf%d" % u, align_bytes=64)
@@ -71,21 +70,22 @@ def tile_picked_yqeq_pair_p_kernel(tc, x_words, x_scales, w1, w2, total, inv, of
             else:
                 nc.scalar.activation(dst, src, ACT.Copy)
             w1_bf.append(wb)
+        w1_codes = sb.tile([P, H], U32, name="w1_codes", align_bytes=64)
+        w1_scales = sb.tile([P, H], U8, name="w1_scales", align_bytes=64)
         for u in range(2):
-            codes = sb.tile([P, 2 * P], U32, name="w1_codes%d" % u, align_bytes=64)
-            scales = sb.tile([P, 2 * P], U8, name="w1_scales%d" % u, align_bytes=64)
-            nc.vector.quantize_mx(out=codes[:].bitcast(FP8X4), scales=scales[:], in_=w1_bf[u][:].rearrange("p t m j -> p (t m j)"))
-            w1_codes.append(codes)
-            w1_scales.append(scales)
+            cols = slice(u * HALF, (u + 1) * HALF)
+            nc.vector.quantize_mx(
+                out=w1_codes[:, cols].bitcast(FP8X4), scales=w1_scales[:, cols], in_=w1_bf[u][:].rearrange("p t m j -> p (t m j)")
+            )
 
-        warm_ps = ps.tile([P, 2 * P], F32, name="warm_ps", tag="bank7")
-        for width in (2 * P, 2 * P, P):
+        warm_ps = ps.tile([64, H], F32, name="warm_ps", tag="bank7")
+        for rep in range(2):
             nc.tensor.matmul_mx(
-                out=warm_ps[:, :width],
-                lhsT=w1_codes[0][:, :P].bitcast(FP8X4),
-                lhsT_scale=w1_scales[0][:, :P],
-                rhs=w1_codes[1][:, :width].bitcast(FP8X4),
-                rhs_scale=w1_scales[1][:, :width],
+                out=warm_ps[:],
+                lhsT=w1_codes[:, :64].bitcast(FP8X4),
+                lhsT_scale=w1_scales[:, :64],
+                rhs=w1_codes[:].bitcast(FP8X4),
+                rhs_scale=w1_scales[:],
                 start=True,
                 stop=True,
             )
@@ -113,11 +113,11 @@ def tile_picked_yqeq_pair_p_kernel(tc, x_words, x_scales, w1, w2, total, inv, of
             hp = ps.tile([P, PACK, CHUNK], F32, name="h_ps%d" % c, tag="bank%d" % c)
             u, o = divmod(c * CHUNK, HALF)
             for t in range(PACK):
-                cols = slice((t % 2) * P, (t % 2 + 1) * P)
+                cols = slice(t * P, (t + 1) * P)
                 nc.tensor.matmul_mx(
                     out=hp[:, t, :],
-                    lhsT=w1_codes[t // 2][:, cols].bitcast(FP8X4),
-                    lhsT_scale=w1_scales[t // 2][:, cols],
+                    lhsT=w1_codes[:, cols].bitcast(FP8X4),
+                    lhsT_scale=w1_scales[:, cols],
                     rhs=xg[u][:, o : o + CHUNK].bitcast(FP8X4),
                     rhs_scale=sg[:, c * CHUNK : (c + 1) * CHUNK],
                     start=True,

@@ -17,9 +17,15 @@ ALU = mybir.AluOpType
 
 P = 128
 PACK = 4
+QUADRANT = 32
 LIST_ROWS = 16
+BANKS = 8
 CHUNK = 128
 HALF = 256
+
+WARM_COLUMNS = 64
+VECTOR_SHARE = 32
+PAIR_RUNS = [(0, 256), (256, 384), (384, 512)]
 
 
 def tile_picked_yqeq_pair_p_kernel(tc, x_words, x_scales, w1, w2, total, inv, offs, pa, pb, out):
@@ -31,152 +37,150 @@ def tile_picked_yqeq_pair_p_kernel(tc, x_words, x_scales, w1, w2, total, inv, of
         offs_sb = sb.tile([P, S // LIST_ROWS], U16, name="offs_sb")
         pa_sb = sb.tile([P, U // LIST_ROWS], U16, name="pa_sb")
         pb_sb = sb.tile([P, U // LIST_ROWS], U16, name="pb_sb")
-        xw = sb.tile([P, T], U32, name="xw", align_bytes=64)
-        xs = sb.tile([P, T], U8, name="xs", align_bytes=64)
+        words_all = sb.tile([P, T], U32, name="words_all", align_bytes=64)
+        scales_all = sb.tile([P, T], U8, name="scales_all", align_bytes=64)
         w1_raw = sb.tile([P, PACK, H], F32, name="w1_raw", align_bytes=64)
         w2_raw = sb.tile([P, PACK, N], F32, name="w2_raw", align_bytes=64)
         total_sb = sb.tile([P, S], F32, name="total_sb", align_bytes=64)
         inv_sb = sb.tile([P, U], F32, name="inv_sb", align_bytes=64)
 
-        nc.vector.memset(xs[:].bitcast(I32), 0)
-        warm = sb.tile([P, 1], F32, name="warm")
+        nc.vector.memset(scales_all[:].bitcast(I32), 0)
+
+        warm_in = sb.tile([P, 1], F32, name="warm_in")
         warm_out = sb.tile([P, 1], F32, name="warm_out")
-        nc.gpsimd.memset(warm[:], 0.0)
-        nc.scalar.activation(warm_out[:], warm[:], ACT.Silu)
+        nc.gpsimd.memset(warm_in[:], 0.0)
+        nc.scalar.activation(warm_out[:], warm_in[:], ACT.Silu)
+
         w1_rows = w1.rearrange("(p j) c -> p j c", j=PACK)
-        nc.sync.dma_start(w1_raw[:, 0:2, :], w1_rows[:, 0:2, :])
+        nc.sync.dma_start(w1_raw[:, : PACK // 2, :], w1_rows[:, : PACK // 2, :])
         nc.sync.dma_start(offs_sb[:], offs)
-        for q in range(4):
-            nc.sync.dma_start(xs[q:P:32, :].bitcast(I32), x_scales[0, q:16:4, :].bitcast(I32))
-        nc.sync.dma_start(w1_raw[:, 2:4, :], w1_rows[:, 2:4, :])
-        nc.sync.dma_start(xw[:].bitcast(I32), x_words[0].rearrange("p n t -> p (n t)").bitcast(I32))
+        for r in range(PACK):
+            nc.sync.dma_start(scales_all[r:P:QUADRANT, :].bitcast(I32), x_scales[0, r : K // 32 : PACK, :].bitcast(I32))
+        nc.sync.dma_start(w1_raw[:, PACK // 2 :, :], w1_rows[:, PACK // 2 :, :])
+        nc.sync.dma_start(words_all[:].bitcast(I32), x_words[0].rearrange("p n t -> p (n t)").bitcast(I32))
         nc.sync.dma_start(w2_raw[:], w2.rearrange("(p j) c -> p j c", j=PACK))
         nc.sync.dma_start(total_sb[:], total)
         nc.sync.dma_start(inv_sb[:], inv)
         nc.sync.dma_start(pa_sb[:], pa)
         nc.sync.dma_start(pb_sb[:], pb)
 
-        sg = sb.tile([P, S], U8, name="sg", align_bytes=64)
-        nc.vector.tensor_copy(sg[:], xs[:].indirect(offs_sb[:]))
+        def offs_half(u):
+            return offs_sb[:, u * HALF // LIST_ROWS : (u + 1) * HALF // LIST_ROWS]
+
+        def pick_scales(u, tag):
+            half = sb.tile([P, HALF], U8, name="x_scales_picked%d" % u, tag=tag, align_bytes=64)
+            nc.vector.tensor_copy(half[:], scales_all[:].indirect(offs_half(u)))
+            return half
+
+        x_scales_picked = [pick_scales(0, "first_scales")]
 
         w1_view = w1_raw[:].rearrange("p j (m t) -> p m j t", t=PACK)
-        w1_bf = []
-        for u in range(2):
-            wb = sb.tile([P, 2, P, PACK], BF16, name="w1_bf%d" % u, align_bytes=64)
-            dst = wb[:].rearrange("p t m j -> p m j t")
-            src = w1_view[:, :, :, 2 * u : 2 * u + 2]
-            if u == 0:
-                nc.vector.tensor_copy(dst, src)
-            else:
-                nc.scalar.activation(dst, src, ACT.Copy)
-            w1_bf.append(wb)
-        w1_codes = sb.tile([P, H], U32, name="w1_codes", align_bytes=64)
+        w1_bf = [sb.tile([P, 2, P, PACK], BF16, name="w1_bf%d" % u, tag="w1_bf%d" % u, align_bytes=64) for u in range(2)]
+        w1_dealt = [pair[:].rearrange("p t m j -> p m j t") for pair in w1_bf]
+        nc.vector.tensor_copy(w1_dealt[0], w1_view[:, :, :, 0:2])
+        nc.vector.tensor_copy(w1_dealt[1][:, :VECTOR_SHARE], w1_view[:, :VECTOR_SHARE, :, 2:4])
+        nc.scalar.activation(w1_dealt[1][:, VECTOR_SHARE:], w1_view[:, VECTOR_SHARE:, :, 2:4], ACT.Copy)
+        w1_words = sb.tile([P, H], U32, name="w1_words", align_bytes=64)
         w1_scales = sb.tile([P, H], U8, name="w1_scales", align_bytes=64)
         for u in range(2):
             cols = slice(u * HALF, (u + 1) * HALF)
             nc.vector.quantize_mx(
-                out=w1_codes[:, cols].bitcast(FP8X4), scales=w1_scales[:, cols], in_=w1_bf[u][:].rearrange("p t m j -> p (t m j)")
+                out=w1_words[:, cols].bitcast(FP8X4), scales=w1_scales[:, cols], in_=w1_bf[u][:].rearrange("p t m j -> p (t m j)")
             )
 
-        warm_ps = ps.tile([64, H], F32, name="warm_ps", tag="bank7")
-        for rep in range(2):
+        x_scales_picked.append(pick_scales(1, "w1_bf0"))
+
+        warm_ps = ps.tile([WARM_COLUMNS, H], F32, name="warm_ps", tag="bank%d" % (BANKS - 1))
+        for warm_pass in range(2):
             nc.tensor.matmul_mx(
                 out=warm_ps[:],
-                lhsT=w1_codes[:, :64].bitcast(FP8X4),
-                lhsT_scale=w1_scales[:, :64],
-                rhs=w1_codes[:].bitcast(FP8X4),
+                lhsT=w1_words[:, :WARM_COLUMNS].bitcast(FP8X4),
+                lhsT_scale=w1_scales[:, :WARM_COLUMNS],
+                rhs=w1_words[:].bitcast(FP8X4),
                 rhs_scale=w1_scales[:],
                 start=True,
                 stop=True,
             )
 
-        xg = []
+        x_words_picked = []
         for u in range(2):
-            g = sb.tile([P, HALF], U32, name="xg%d" % u, align_bytes=64)
-            nc.vector.tensor_copy(g[:], xw[:].indirect(offs_sb[:, 16 * u : 16 * u + 16]))
-            xg.append(g)
+            half = sb.tile([P, HALF], U32, name="x_words_picked%d" % u, align_bytes=64)
+            nc.vector.tensor_copy(half[:], words_all[:].indirect(offs_half(u)))
+            x_words_picked.append(half)
 
         w2_bf = sb.tile([P, N, PACK], BF16, name="w2_bf", align_bytes=64)
         nc.scalar.activation(
             w2_bf[:].rearrange("p (c i) j -> p c j i", i=4), w2_raw[:].rearrange("p j (c i) -> p c j i", i=4), ACT.Copy
         )
-        w2_codes = sb.tile([P, N], U32, name="w2_codes", align_bytes=64)
+        w2_words = sb.tile([P, N], U32, name="w2_words", align_bytes=64)
         w2_scales = sb.tile([P, N], U8, name="w2_scales", align_bytes=64)
-        nc.vector.quantize_mx(out=w2_codes[:].bitcast(FP8X4), scales=w2_scales[:], in_=w2_bf[:].rearrange("p n j -> p (n j)"))
+        nc.vector.quantize_mx(out=w2_words[:].bitcast(FP8X4), scales=w2_scales[:], in_=w2_bf[:].rearrange("p n j -> p (n j)"))
 
-        nbanks = S // CHUNK
-        pieces = [(0, 128), (128, 256), (256, 384), (384, 512)]
+        chunks = S // CHUNK
         ch = sb.tile([P, S], F32, name="ch", align_bytes=64)
         h_ps, h_bf, y_ps, sums, shifted = [], {}, {}, {}, {}
 
-        def layer1(c):
-            hp = ps.tile([P, PACK, CHUNK], F32, name="h_ps%d" % c, tag="bank%d" % c)
-            u, o = divmod(c * CHUNK, HALF)
+        def first_product(c):
+            bank = ps.tile([P, PACK, CHUNK], F32, name="h_ps%d" % c, tag="bank%d" % c)
+            u, start = divmod(c * CHUNK, HALF)
             for t in range(PACK):
                 cols = slice(t * P, (t + 1) * P)
                 nc.tensor.matmul_mx(
-                    out=hp[:, t, :],
-                    lhsT=w1_codes[:, cols].bitcast(FP8X4),
+                    out=bank[:, t, :],
+                    lhsT=w1_words[:, cols].bitcast(FP8X4),
                     lhsT_scale=w1_scales[:, cols],
-                    rhs=xg[u][:, o : o + CHUNK].bitcast(FP8X4),
-                    rhs_scale=sg[:, c * CHUNK : (c + 1) * CHUNK],
+                    rhs=x_words_picked[u][:, start : start + CHUNK].bitcast(FP8X4),
+                    rhs_scale=x_scales_picked[u][:, start : start + CHUNK],
                     start=True,
                     stop=True,
                 )
-            h_ps.append(hp)
+            h_ps.append(bank)
 
-        def act(i):
-            lo, hi = pieces[i]
-            c, o = divmod(lo, CHUNK)
-            hb = sb.tile([P, hi - lo, PACK], BF16, name="h_bf%d" % i, align_bytes=64)
-            nc.scalar.activation(hb[:], h_ps[c][:, :, o : o + hi - lo].rearrange("p t n -> p n t"), ACT.Silu)
-            h_bf[i] = hb
+        def silu(c):
+            h_bf[c] = sb.tile([P, CHUNK, PACK], BF16, name="h_bf%d" % c, align_bytes=64)
+            nc.scalar.activation(h_bf[c][:], h_ps[c][:].rearrange("p t n -> p n t"), ACT.Silu)
 
-        def layer2(i):
-            lo, hi = pieces[i]
-            codes = sb.tile([P, hi - lo], U32, name="h_codes%d" % i, align_bytes=64)
-            scales = sb.tile([P, hi - lo], U8, name="h_scales%d" % i, align_bytes=64)
-            nc.vector.quantize_mx(out=codes[:].bitcast(FP8X4), scales=scales[:], in_=h_bf[i][:].rearrange("p n t -> p (n t)"))
-            yp = ps.tile([P, hi - lo], F32, name="y_ps%d" % i, tag="bank%d" % ((nbanks + i) % 8))
+        def second_product(c):
+            h_words = sb.tile([P, CHUNK], U32, name="h_words%d" % c, align_bytes=64)
+            h_scales = sb.tile([P, CHUNK], U8, name="h_scales%d" % c, align_bytes=64)
+            nc.vector.quantize_mx(out=h_words[:].bitcast(FP8X4), scales=h_scales[:], in_=h_bf[c][:].rearrange("p n t -> p (n t)"))
+            y_ps[c] = ps.tile([P, CHUNK], F32, name="y_ps%d" % c, tag="bank%d" % (chunks + c))
             nc.tensor.matmul_mx(
-                out=yp[:],
-                lhsT=w2_codes[:].bitcast(FP8X4),
+                out=y_ps[c][:],
+                lhsT=w2_words[:].bitcast(FP8X4),
                 lhsT_scale=w2_scales[:],
-                rhs=codes[:].bitcast(FP8X4),
-                rhs_scale=scales[:],
+                rhs=h_words[:].bitcast(FP8X4),
+                rhs_scale=h_scales[:],
                 start=True,
                 stop=True,
             )
-            y_ps[i] = yp
 
-        def read_y(i):
-            lo, hi = pieces[i]
-            sums[i] = sb.tile([P, (hi - lo) // D], F32, name="sums%d" % i)
-            nc.vector.tensor_reduce(sums[i][:], y_ps[i][:].rearrange("p (v d) -> p v d", d=D), mybir.AxisListType.X, ALU.add)
-            shifted[i] = sb.tile([P, hi - lo], F32, name="shifted%d" % i)
-            nc.vector.tensor_tensor(shifted[i][:], y_ps[i][:], total_sb[:, lo:hi], ALU.add)
+        def read_y(c):
+            sums[c] = sb.tile([P, CHUNK // D], F32, name="sums%d" % c)
+            nc.vector.tensor_reduce(sums[c][:], y_ps[c][:].rearrange("p (v d) -> p v d", d=D), mybir.AxisListType.X, ALU.add)
+            shifted[c] = sb.tile([P, CHUNK], F32, name="shifted%d" % c)
+            nc.vector.tensor_tensor(shifted[c][:], y_ps[c][:], total_sb[:, c * CHUNK : (c + 1) * CHUNK], ALU.add)
 
-        def centre(i):
-            lo, hi = pieces[i]
+        def centre(c):
             nc.vector.scalar_tensor_tensor(
-                ch[:, lo:hi].rearrange("p (v d) -> p v d", d=D),
-                sums[i][:].unsqueeze(2).to_broadcast([P, (hi - lo) // D, D]),
+                ch[:, c * CHUNK : (c + 1) * CHUNK].rearrange("p (v d) -> p v d", d=D),
+                sums[c][:].unsqueeze(2).to_broadcast([P, CHUNK // D, D]),
                 -1.0 / D,
-                shifted[i][:].rearrange("p (v d) -> p v d", d=D),
+                shifted[c][:].rearrange("p (v d) -> p v d", d=D),
                 ALU.mult,
                 ALU.add,
             )
 
-        for c in range(nbanks):
-            layer1(c)
-        for i in range(len(pieces)):
-            act(i)
-        layer2(0)
-        layer2(1)
+        for c in range(chunks):
+            first_product(c)
+        for c in range(chunks):
+            silu(c)
+        second_product(0)
+        second_product(1)
         read_y(0)
-        layer2(2)
+        second_product(2)
         centre(0)
-        layer2(3)
+        second_product(3)
         read_y(1)
         read_y(2)
         centre(1)
@@ -186,16 +190,15 @@ def tile_picked_yqeq_pair_p_kernel(tc, x_words, x_scales, w1, w2, total, inv, of
 
         left = []
         for u in range(2):
-            cols = slice(u * HALF, (u + 1) * HALF)
-            a = sb.tile([P, HALF], F32, name="left%d" % u)
-            nc.vector.tensor_tensor(a[:], ch[:].indirect(pa_sb[:, 16 * u : 16 * u + 16]), inv_sb[:, cols], ALU.mult)
-            left.append(a)
-        for lo, hi in ((0, 256), (256, 384), (384, 512)):
-            u, o = divmod(lo, HALF)
+            factor = sb.tile([P, HALF], F32, name="left%d" % u)
+            entries = pa_sb[:, u * HALF // LIST_ROWS : (u + 1) * HALF // LIST_ROWS]
+            nc.vector.tensor_tensor(factor[:], ch[:].indirect(entries), inv_sb[:, u * HALF : (u + 1) * HALF], ALU.mult)
+            left.append(factor)
+        for lo, hi in PAIR_RUNS:
+            u, start = divmod(lo, HALF)
             prod = sb.tile([P, hi - lo], F32, name="prod%d" % lo)
-            nc.vector.tensor_tensor(
-                prod[:], ch[:].indirect(pb_sb[:, lo // LIST_ROWS : hi // LIST_ROWS]), left[u][:, o : o + hi - lo], ALU.mult
-            )
+            entries = pb_sb[:, lo // LIST_ROWS : hi // LIST_ROWS]
+            nc.vector.tensor_tensor(prod[:], ch[:].indirect(entries), left[u][:, start : start + hi - lo], ALU.mult)
             res = sb.tile([P, hi - lo], F32, name="res%d" % lo)
             nc.scalar.activation(res[:], prod[:], ACT.Tanh)
             nc.sync.dma_start(out[:, lo:hi], res[:])

@@ -18,6 +18,7 @@ ALU = mybir.AluOpType
 P = 128
 PACK = 4
 QUADRANT = 32
+BLOCK_ROWS = 8
 LIST_ROWS = 16
 BANKS = 8
 CHUNK = 128
@@ -38,13 +39,12 @@ def tile_picked_yqeq_pair_p_kernel(tc, x_words, x_scales, w1, w2, total, inv, of
         pa_sb = sb.tile([P, U // LIST_ROWS], U16, name="pa_sb")
         pb_sb = sb.tile([P, U // LIST_ROWS], U16, name="pb_sb")
         words_all = sb.tile([P, T], U32, name="words_all", align_bytes=64)
-        scales_all = sb.tile([P, T], U8, name="scales_all", align_bytes=64)
-        w1_raw = sb.tile([P, PACK, H], F32, name="w1_raw", align_bytes=64)
-        w2_raw = sb.tile([P, PACK, N], F32, name="w2_raw", align_bytes=64)
-        total_sb = sb.tile([P, S], F32, name="total_sb", align_bytes=64)
-        inv_sb = sb.tile([P, U], F32, name="inv_sb", align_bytes=64)
+        scales_all = sb.tile([P, T], U8, name="scales_all", tag="scales_all", align_bytes=64)
+        w1_raw = sb.tile([P, PACK, H], F32, name="w1_raw", tag="w1_raw", align_bytes=64)
+        x_scales_placed = sb.tile([P, S], U8, name="x_scales_placed", align_bytes=64)
 
         nc.vector.memset(scales_all[:].bitcast(I32), 0)
+        nc.gpsimd.memset(x_scales_placed[:].bitcast(I32), 0)
 
         warm_in = sb.tile([P, 1], F32, name="warm_in")
         warm_out = sb.tile([P, 1], F32, name="warm_out")
@@ -54,25 +54,23 @@ def tile_picked_yqeq_pair_p_kernel(tc, x_words, x_scales, w1, w2, total, inv, of
         w1_rows = w1.rearrange("(p j) c -> p j c", j=PACK)
         nc.sync.dma_start(w1_raw[:, : PACK // 2, :], w1_rows[:, : PACK // 2, :])
         nc.sync.dma_start(offs_sb[:], offs)
-        for r in range(PACK):
-            nc.sync.dma_start(scales_all[r:P:QUADRANT, :].bitcast(I32), x_scales[0, r : K // 32 : PACK, :].bitcast(I32))
+        nc.sync.dma_start(scales_all[0:P:BLOCK_ROWS, :].bitcast(I32), x_scales[0].bitcast(I32))
         nc.sync.dma_start(w1_raw[:, PACK // 2 :, :], w1_rows[:, PACK // 2 :, :])
         nc.sync.dma_start(words_all[:].bitcast(I32), x_words[0].rearrange("p n t -> p (n t)").bitcast(I32))
-        nc.sync.dma_start(w2_raw[:], w2.rearrange("(p j) c -> p j c", j=PACK))
-        nc.sync.dma_start(total_sb[:], total)
-        nc.sync.dma_start(inv_sb[:], inv)
         nc.sync.dma_start(pa_sb[:], pa)
         nc.sync.dma_start(pb_sb[:], pb)
 
         def offs_half(u):
             return offs_sb[:, u * HALF // LIST_ROWS : (u + 1) * HALF // LIST_ROWS]
 
-        def pick_scales(u, tag):
-            half = sb.tile([P, HALF], U8, name="x_scales_picked%d" % u, tag=tag, align_bytes=64)
-            nc.vector.tensor_copy(half[:], scales_all[:].indirect(offs_half(u)))
-            return half
-
-        x_scales_picked = [pick_scales(0, "first_scales")]
+        x_scales_picked = sb.tile([P, S], U8, name="x_scales_picked", align_bytes=64)
+        nc.vector.tensor_copy(x_scales_picked[:], scales_all[:].indirect(offs_sb[:]))
+        for r in range(PACK):
+            nc.sync.dma_start(
+                x_scales_placed[r:P:QUADRANT, :].bitcast(I32), x_scales_picked[r * BLOCK_ROWS : P : QUADRANT, :].bitcast(I32)
+            )
+        w2_raw = sb.tile([P, PACK, N], F32, name="w2_raw", tag="scales_all", align_bytes=64)
+        nc.sync.dma_start(w2_raw[:], w2.rearrange("(p j) c -> p j c", j=PACK))
 
         w1_view = w1_raw[:].rearrange("p j (m t) -> p m j t", t=PACK)
         w1_bf = [sb.tile([P, 2, P, PACK], BF16, name="w1_bf%d" % u, tag="w1_bf%d" % u, align_bytes=64) for u in range(2)]
@@ -88,7 +86,10 @@ def tile_picked_yqeq_pair_p_kernel(tc, x_words, x_scales, w1, w2, total, inv, of
                 out=w1_words[:, cols].bitcast(FP8X4), scales=w1_scales[:, cols], in_=w1_bf[u][:].rearrange("p t m j -> p (t m j)")
             )
 
-        x_scales_picked.append(pick_scales(1, "w1_bf0"))
+        rows_sb = sb.tile([P, 2, S], F32, name="rows_sb", tag="w1_raw", align_bytes=64)
+        total_sb, inv_sb = rows_sb[:, 0, :], rows_sb[:, 1, :]
+        nc.sync.dma_start(total_sb, total)
+        nc.sync.dma_start(inv_sb, inv)
 
         warm_ps = ps.tile([WARM_COLUMNS, H], F32, name="warm_ps", tag="bank%d" % (BANKS - 1))
         for warm_pass in range(2):
@@ -109,9 +110,7 @@ def tile_picked_yqeq_pair_p_kernel(tc, x_words, x_scales, w1, w2, total, inv, of
             x_words_picked.append(half)
 
         w2_bf = sb.tile([P, N, PACK], BF16, name="w2_bf", align_bytes=64)
-        nc.scalar.activation(
-            w2_bf[:].rearrange("p (c i) j -> p c j i", i=4), w2_raw[:].rearrange("p j (c i) -> p c j i", i=4), ACT.Copy
-        )
+        nc.vector.tensor_copy(w2_bf[:].rearrange("p (c i) j -> p c j i", i=4), w2_raw[:].rearrange("p j (c i) -> p c j i", i=4))
         w2_words = sb.tile([P, N], U32, name="w2_words", align_bytes=64)
         w2_scales = sb.tile([P, N], U8, name="w2_scales", align_bytes=64)
         nc.vector.quantize_mx(out=w2_words[:].bitcast(FP8X4), scales=w2_scales[:], in_=w2_bf[:].rearrange("p n j -> p (n j)"))
@@ -130,7 +129,7 @@ def tile_picked_yqeq_pair_p_kernel(tc, x_words, x_scales, w1, w2, total, inv, of
                     lhsT=w1_words[:, cols].bitcast(FP8X4),
                     lhsT_scale=w1_scales[:, cols],
                     rhs=x_words_picked[u][:, start : start + CHUNK].bitcast(FP8X4),
-                    rhs_scale=x_scales_picked[u][:, start : start + CHUNK],
+                    rhs_scale=x_scales_placed[:, c * CHUNK : (c + 1) * CHUNK],
                     start=True,
                     stop=True,
                 )

@@ -20,11 +20,9 @@ PACK = 4
 QUADRANT = 32
 BLOCK_ROWS = 8
 LIST_ROWS = 16
-BANKS = 8
 CHUNK = 128
 HALF = 256
 
-WARM_COLUMNS = 64
 VECTOR_SHARE = 32
 PAIR_RUNS = [(0, 256), (256, 384), (384, 512)]
 
@@ -90,18 +88,6 @@ def tile_picked_yqeq_pair_p_kernel(tc, x_words, x_scales, w1, w2, total, inv, of
         total_sb, inv_sb = rows_sb[:, 0, :], rows_sb[:, 1, :]
         nc.sync.dma_start(total_sb, total)
         nc.sync.dma_start(inv_sb, inv)
-
-        warm_ps = ps.tile([WARM_COLUMNS, H], F32, name="warm_ps", tag="bank%d" % (BANKS - 1))
-        for warm_pass in range(2):
-            nc.tensor.matmul_mx(
-                out=warm_ps[:],
-                lhsT=w1_words[:, :WARM_COLUMNS].bitcast(FP8X4),
-                lhsT_scale=w1_scales[:, :WARM_COLUMNS],
-                rhs=w1_words[:].bitcast(FP8X4),
-                rhs_scale=w1_scales[:],
-                start=True,
-                stop=True,
-            )
 
         x_words_picked = []
         for u in range(2):

@@ -20,10 +20,12 @@ PACK = 4
 QUADRANT = 32
 BLOCK_ROWS = 8
 LIST_ROWS = 16
+BANKS = 8
 CHUNK = 128
 HALF = 256
 
 VECTOR_SHARE = 32
+PIECES = [(0, 128), (128, 256), (256, 384), (384, 448), (448, 512)]
 PAIR_RUNS = [(0, 256), (256, 384), (384, 512)]
 
 
@@ -122,14 +124,17 @@ def tile_picked_yqeq_pair_p_kernel(tc, x_words, x_scales, w1, w2, total, inv, of
             h_ps.append(bank)
 
         def silu(c):
-            h_bf[c] = sb.tile([P, CHUNK, PACK], BF16, name="h_bf%d" % c, align_bytes=64)
-            nc.scalar.activation(h_bf[c][:], h_ps[c][:].rearrange("p t n -> p n t"), ACT.Silu)
+            lo, hi = PIECES[c]
+            bank, start = divmod(lo, CHUNK)
+            h_bf[c] = sb.tile([P, hi - lo, PACK], BF16, name="h_bf%d" % c, align_bytes=64)
+            nc.scalar.activation(h_bf[c][:], h_ps[bank][:, :, start : start + hi - lo].rearrange("p t n -> p n t"), ACT.Silu)
 
         def second_product(c):
-            h_words = sb.tile([P, CHUNK], U32, name="h_words%d" % c, align_bytes=64)
-            h_scales = sb.tile([P, CHUNK], U8, name="h_scales%d" % c, align_bytes=64)
+            lo, hi = PIECES[c]
+            h_words = sb.tile([P, hi - lo], U32, name="h_words%d" % c, align_bytes=64)
+            h_scales = sb.tile([P, hi - lo], U8, name="h_scales%d" % c, align_bytes=64)
             nc.vector.quantize_mx(out=h_words[:].bitcast(FP8X4), scales=h_scales[:], in_=h_bf[c][:].rearrange("p n t -> p (n t)"))
-            y_ps[c] = ps.tile([P, CHUNK], F32, name="y_ps%d" % c, tag="bank%d" % (chunks + c))
+            y_ps[c] = ps.tile([P, hi - lo], F32, name="y_ps%d" % c, tag="bank%d" % ((chunks + c) % BANKS))
             nc.tensor.matmul_mx(
                 out=y_ps[c][:],
                 lhsT=w2_words[:].bitcast(FP8X4),
@@ -141,15 +146,17 @@ def tile_picked_yqeq_pair_p_kernel(tc, x_words, x_scales, w1, w2, total, inv, of
             )
 
         def read_y(c):
-            sums[c] = sb.tile([P, CHUNK // D], F32, name="sums%d" % c)
+            lo, hi = PIECES[c]
+            sums[c] = sb.tile([P, (hi - lo) // D], F32, name="sums%d" % c)
             nc.vector.tensor_reduce(sums[c][:], y_ps[c][:].rearrange("p (v d) -> p v d", d=D), mybir.AxisListType.X, ALU.add)
-            shifted[c] = sb.tile([P, CHUNK], F32, name="shifted%d" % c)
-            nc.vector.tensor_tensor(shifted[c][:], y_ps[c][:], total_sb[:, c * CHUNK : (c + 1) * CHUNK], ALU.add)
+            shifted[c] = sb.tile([P, hi - lo], F32, name="shifted%d" % c)
+            nc.vector.tensor_tensor(shifted[c][:], y_ps[c][:], total_sb[:, lo:hi], ALU.add)
 
         def centre(c):
+            lo, hi = PIECES[c]
             nc.vector.scalar_tensor_tensor(
-                ch[:, c * CHUNK : (c + 1) * CHUNK].rearrange("p (v d) -> p v d", d=D),
-                sums[c][:].unsqueeze(2).to_broadcast([P, CHUNK // D, D]),
+                ch[:, lo:hi].rearrange("p (v d) -> p v d", d=D),
+                sums[c][:].unsqueeze(2).to_broadcast([P, (hi - lo) // D, D]),
                 -1.0 / D,
                 shifted[c][:].rearrange("p (v d) -> p v d", d=D),
                 ALU.mult,
@@ -158,7 +165,7 @@ def tile_picked_yqeq_pair_p_kernel(tc, x_words, x_scales, w1, w2, total, inv, of
 
         for c in range(chunks):
             first_product(c)
-        for c in range(chunks):
+        for c in range(len(PIECES)):
             silu(c)
         second_product(0)
         second_product(1)
@@ -166,12 +173,15 @@ def tile_picked_yqeq_pair_p_kernel(tc, x_words, x_scales, w1, w2, total, inv, of
         second_product(2)
         centre(0)
         second_product(3)
+        second_product(4)
         read_y(1)
         read_y(2)
         centre(1)
         read_y(3)
+        read_y(4)
         centre(2)
         centre(3)
+        centre(4)
 
         left = []
         for u in range(2):

@@ -25,6 +25,7 @@ CHUNK = 128
 HALF = 256
 
 VECTOR_SHARE = 32
+W1_FIRST = 768
 PIECES = [(0, 128), (128, 256), (256, 384), (384, 448), (448, 512)]
 PAIR_RUNS = [(0, 256), (256, 384), (384, 512)]
 
@@ -39,23 +40,23 @@ def tile_picked_yqeq_pair_p_kernel(tc, x_words, x_scales, w1, w2, total, inv, of
         pa_sb = sb.tile([P, U // LIST_ROWS], U16, name="pa_sb")
         pb_sb = sb.tile([P, U // LIST_ROWS], U16, name="pb_sb")
         words_all = sb.tile([P, T], U32, name="words_all", align_bytes=64)
-        scales_all = sb.tile([P, T], U8, name="scales_all", tag="scales_all", align_bytes=64)
+        scales_all = sb.tile([P, T], U8, name="scales_all", align_bytes=64)
         w1_raw = sb.tile([P, PACK, H], F32, name="w1_raw", tag="w1_raw", align_bytes=64)
         x_scales_placed = sb.tile([P, S], U8, name="x_scales_placed", align_bytes=64)
 
         nc.vector.memset(scales_all[:].bitcast(I32), 0)
-        nc.gpsimd.memset(x_scales_placed[:].bitcast(I32), 0)
 
         warm_in = sb.tile([P, 1], F32, name="warm_in")
         warm_out = sb.tile([P, 1], F32, name="warm_out")
         nc.gpsimd.memset(warm_in[:], 0.0)
         nc.scalar.activation(warm_out[:], warm_in[:], ACT.Silu)
 
-        w1_rows = w1.rearrange("(p j) c -> p j c", j=PACK)
-        nc.sync.dma_start(w1_raw[:, : PACK // 2, :], w1_rows[:, : PACK // 2, :])
+        w1_rows = w1.rearrange("(p j) c -> p (j c)", j=PACK)
+        w1_flat = w1_raw[:].rearrange("p j c -> p (j c)")
+        nc.sync.dma_start(w1_flat[:, :W1_FIRST], w1_rows[:, :W1_FIRST])
         nc.sync.dma_start(offs_sb[:], offs)
         nc.sync.dma_start(scales_all[0:P:BLOCK_ROWS, :].bitcast(I32), x_scales[0].bitcast(I32))
-        nc.sync.dma_start(w1_raw[:, PACK // 2 :, :], w1_rows[:, PACK // 2 :, :])
+        nc.sync.dma_start(w1_flat[:, W1_FIRST:], w1_rows[:, W1_FIRST:])
         nc.sync.dma_start(words_all[:].bitcast(I32), x_words[0].rearrange("p n t -> p (n t)").bitcast(I32))
         nc.sync.dma_start(pa_sb[:], pa)
         nc.sync.dma_start(pb_sb[:], pb)
@@ -65,12 +66,11 @@ def tile_picked_yqeq_pair_p_kernel(tc, x_words, x_scales, w1, w2, total, inv, of
 
         x_scales_picked = sb.tile([P, S], U8, name="x_scales_picked", align_bytes=64)
         nc.vector.tensor_copy(x_scales_picked[:], scales_all[:].indirect(offs_sb[:]))
-        for r in range(PACK):
+        nc.vector.tensor_copy(x_scales_placed[:].bitcast(I32), x_scales_picked[:].bitcast(I32))
+        for r in range(1, PACK):
             nc.sync.dma_start(
                 x_scales_placed[r:P:QUADRANT, :].bitcast(I32), x_scales_picked[r * BLOCK_ROWS : P : QUADRANT, :].bitcast(I32)
             )
-        w2_raw = sb.tile([P, PACK, N], F32, name="w2_raw", tag="scales_all", align_bytes=64)
-        nc.sync.dma_start(w2_raw[:], w2.rearrange("(p j) c -> p j c", j=PACK))
 
         w1_view = w1_raw[:].rearrange("p j (m t) -> p m j t", t=PACK)
         w1_bf = [sb.tile([P, 2, P, PACK], BF16, name="w1_bf%d" % u, tag="w1_bf%d" % u, align_bytes=64) for u in range(2)]
@@ -86,8 +86,9 @@ def tile_picked_yqeq_pair_p_kernel(tc, x_words, x_scales, w1, w2, total, inv, of
                 out=w1_words[:, cols].bitcast(FP8X4), scales=w1_scales[:, cols], in_=w1_bf[u][:].rearrange("p t m j -> p (t m j)")
             )
 
-        rows_sb = sb.tile([P, 2, S], F32, name="rows_sb", tag="w1_raw", align_bytes=64)
-        total_sb, inv_sb = rows_sb[:, 0, :], rows_sb[:, 1, :]
+        late = sb.tile([P, 3 * S], F32, name="late", tag="w1_raw", align_bytes=64)
+        w2_raw, total_sb, inv_sb = late[:, :S], late[:, S : 2 * S], late[:, 2 * S :]
+        nc.sync.dma_start(w2_raw, w2.rearrange("(p j) c -> p (j c)", j=PACK))
         nc.sync.dma_start(total_sb, total)
         nc.sync.dma_start(inv_sb, inv)
 
@@ -98,7 +99,7 @@ def tile_picked_yqeq_pair_p_kernel(tc, x_words, x_scales, w1, w2, total, inv, of
             x_words_picked.append(half)
 
         w2_bf = sb.tile([P, N, PACK], BF16, name="w2_bf", align_bytes=64)
-        nc.vector.tensor_copy(w2_bf[:].rearrange("p (c i) j -> p c j i", i=4), w2_raw[:].rearrange("p j (c i) -> p c j i", i=4))
+        nc.vector.tensor_copy(w2_bf[:].rearrange("p (c i) j -> p c j i", i=4), w2_raw.rearrange("p (j c i) -> p c j i", j=PACK, i=4))
         w2_words = sb.tile([P, N], U32, name="w2_words", align_bytes=64)
         w2_scales = sb.tile([P, N], U8, name="w2_scales", align_bytes=64)
         nc.vector.quantize_mx(out=w2_words[:].bitcast(FP8X4), scales=w2_scales[:], in_=w2_bf[:].rearrange("p n j -> p (n j)"))

@@ -77,7 +77,8 @@ def tile_picked_yqeq_pair_p_kernel(tc, x_words, x_scales, w1, w2, total, inv, of
         w1_dealt = [pair[:].rearrange("p t m j -> p m j t") for pair in w1_bf]
         nc.vector.tensor_copy(w1_dealt[0], w1_view[:, :, :, 0:2])
         nc.vector.tensor_copy(w1_dealt[1][:, :VECTOR_SHARE], w1_view[:, :VECTOR_SHARE, :, 2:4])
-        nc.scalar.activation(w1_dealt[1][:, VECTOR_SHARE:], w1_view[:, VECTOR_SHARE:, :, 2:4], ACT.Copy)
+        for lo, hi in ((VECTOR_SHARE, (VECTOR_SHARE + P) // 2), ((VECTOR_SHARE + P) // 2, P)):
+            nc.scalar.activation(w1_dealt[1][:, lo:hi], w1_view[:, lo:hi, :, 2:4], ACT.Copy)
         w1_words = sb.tile([P, H], U32, name="w1_words", align_bytes=64)
         w1_scales = sb.tile([P, H], U8, name="w1_scales", align_bytes=64)
         for u in range(2):

@@ -107,83 +107,90 @@ def tile_picked_yqeq_pair_p_kernel(tc, x_words, x_scales, w1, w2, total, inv, of
 
         chunks = S // CHUNK
         ch = sb.tile([P, S], F32, name="ch", align_bytes=64)
-        h_ps, h_bf, y_ps, sums, shifted = [], {}, {}, {}, {}
+        sums = sb.tile([P, S // D], F32, name="sums")
+        shifted = sb.tile([P, S], F32, name="shifted")
+        h_ps, h_bf, y_ps = [], {}, {}
 
-        def first_product(c):
-            bank = ps.tile([P, PACK, CHUNK], F32, name="h_ps%d" % c, tag="bank%d" % c)
+        shared_scales = sb.tile([P, CHUNK], U8, name="shared_scales", align_bytes=64)
+        nc.vector.tensor_copy(shared_scales[:].bitcast(I32), x_scales_placed[:, S - CHUNK :].bitcast(I32))
+
+        def first_product(c, operands):
+            if c == len(h_ps):
+                h_ps.append(ps.tile([P, PACK, CHUNK], F32, name="h_ps%d" % c, tag="bank%d" % c))
+            bank = h_ps[c]
             u, start = divmod(c * CHUNK, HALF)
-            for t in range(PACK):
+            for t in operands:
                 cols = slice(t * P, (t + 1) * P)
                 nc.tensor.matmul_mx(
                     out=bank[:, t, :],
                     lhsT=w1_words[:, cols].bitcast(FP8X4),
                     lhsT_scale=w1_scales[:, cols],
                     rhs=x_words_picked[u][:, start : start + CHUNK].bitcast(FP8X4),
-                    rhs_scale=x_scales_placed[:, c * CHUNK : (c + 1) * CHUNK],
+                    rhs_scale=shared_scales[:] if (c, t) == (chunks - 1, PACK - 1) else x_scales_placed[:, c * CHUNK : (c + 1) * CHUNK],
                     start=True,
                     stop=True,
                 )
-            h_ps.append(bank)
 
         def silu(c):
             lo, hi = PIECES[c]
             bank, start = divmod(lo, CHUNK)
-            h_bf[c] = sb.tile([P, hi - lo, PACK], BF16, name="h_bf%d" % c, align_bytes=64)
+            h_bf[c] = sb.tile([P, hi - lo, PACK], BF16, name="h_bf%d" % c, tag="h_bf%d" % c, align_bytes=64)
             nc.scalar.activation(h_bf[c][:], h_ps[bank][:, :, start : start + hi - lo].rearrange("p t n -> p n t"), ACT.Silu)
 
         def second_product(c):
             lo, hi = PIECES[c]
             h_words = sb.tile([P, hi - lo], U32, name="h_words%d" % c, align_bytes=64)
-            h_scales = sb.tile([P, hi - lo], U8, name="h_scales%d" % c, align_bytes=64)
-            nc.vector.quantize_mx(out=h_words[:].bitcast(FP8X4), scales=h_scales[:], in_=h_bf[c][:].rearrange("p n t -> p (n t)"))
-            y_ps[c] = ps.tile([P, hi - lo], F32, name="y_ps%d" % c, tag="bank%d" % ((chunks + c) % BANKS))
+            h_scales = shared_scales[PACK:, :] if c == 0 else sb.tile([P, hi - lo], U8, name="h_scales%d" % c, align_bytes=64)[:]
+            nc.vector.quantize_mx(out=h_words[:].bitcast(FP8X4), scales=h_scales, in_=h_bf[c][:].rearrange("p n t -> p (n t)"))
+            y_ps[c] = ps.tile([P, hi - lo], F32, name="y_ps%d" % c, tag="bank%d" % [4, 2, 5, 6, 7][c])
             nc.tensor.matmul_mx(
                 out=y_ps[c][:],
                 lhsT=w2_words[:].bitcast(FP8X4),
                 lhsT_scale=w2_scales[:],
                 rhs=h_words[:].bitcast(FP8X4),
-                rhs_scale=h_scales[:],
+                rhs_scale=h_scales,
                 start=True,
                 stop=True,
             )
 
-        def read_y(c):
+        def sum_y(c):
             lo, hi = PIECES[c]
-            sums[c] = sb.tile([P, (hi - lo) // D], F32, name="sums%d" % c)
-            nc.vector.tensor_reduce(sums[c][:], y_ps[c][:].rearrange("p (v d) -> p v d", d=D), mybir.AxisListType.X, ALU.add)
-            shifted[c] = sb.tile([P, hi - lo], F32, name="shifted%d" % c)
-            nc.vector.tensor_tensor(shifted[c][:], y_ps[c][:], total_sb[:, lo:hi], ALU.add)
+            nc.vector.tensor_reduce(sums[:, lo // D : hi // D], y_ps[c][:].rearrange("p (v d) -> p v d", d=D), mybir.AxisListType.X, ALU.add)
 
-        def centre(c):
+        def shift_y(c):
             lo, hi = PIECES[c]
+            nc.vector.tensor_tensor(shifted[:, lo:hi], y_ps[c][:], total_sb[:, lo:hi], ALU.add)
+
+        def centre(lo, hi):
             nc.vector.scalar_tensor_tensor(
                 ch[:, lo:hi].rearrange("p (v d) -> p v d", d=D),
-                sums[c][:].unsqueeze(2).to_broadcast([P, (hi - lo) // D, D]),
+                sums[:, lo // D : hi // D].unsqueeze(2).to_broadcast([P, (hi - lo) // D, D]),
                 -1.0 / D,
-                shifted[c][:].rearrange("p (v d) -> p v d", d=D),
+                shifted[:, lo:hi].rearrange("p (v d) -> p v d", d=D),
                 ALU.mult,
                 ALU.add,
             )
 
-        for c in range(chunks):
-            first_product(c)
-        for c in range(len(PIECES)):
-            silu(c)
+        for c in range(chunks - 1):
+            first_product(c, range(PACK))
+        first_product(chunks - 1, range(PACK - 1))
+        silu(0)
         second_product(0)
-        second_product(1)
-        read_y(0)
-        second_product(2)
-        centre(0)
-        second_product(3)
-        second_product(4)
-        read_y(1)
-        read_y(2)
-        centre(1)
-        read_y(3)
-        read_y(4)
-        centre(2)
-        centre(3)
-        centre(4)
+        first_product(chunks - 1, [PACK - 1])
+        for c in range(1, len(PIECES)):
+            silu(c)
+        for c in range(1, len(PIECES)):
+            second_product(c)
+        sum_y(0)
+        shift_y(0)
+        sum_y(1)
+        centre(*PIECES[0])
+        shift_y(1)
+        for c in range(2, len(PIECES)):
+            sum_y(c)
+            shift_y(c)
+        centre(PIECES[1][0], PIECES[-2][1])
+        centre(*PIECES[-1])
 
         left = []
         for u in range(2):

@@ -87,6 +87,18 @@ def tile_picked_yqeq_pair_p_kernel(tc, x_words, x_scales, w1, w2, total, inv, of
                 out=w1_words[:, cols].bitcast(FP8X4), scales=w1_scales[:, cols], in_=w1_bf[u][:].rearrange("p t m j -> p (t m j)")
             )
 
+        for u, width in enumerate((H, P)):
+            pe_warm = ps.tile([P, width], F32, name="pe_warm%d" % u, tag="bank%d" % (BANKS - 1 - u))
+            nc.tensor.matmul_mx(
+                out=pe_warm[:],
+                lhsT=w1_words[:, :P].bitcast(FP8X4),
+                lhsT_scale=w1_scales[:, :P],
+                rhs=w1_words[:, :width].bitcast(FP8X4),
+                rhs_scale=w1_scales[:, :width],
+                start=True,
+                stop=True,
+            )
+
         late = sb.tile([P, 3 * S], F32, name="late", tag="w1_raw", align_bytes=64)
         w2_raw, total_sb, inv_sb = late[:, :S], late[:, S : 2 * S], late[:, 2 * S :]
         nc.sync.dma_start(w2_raw, w2.rearrange("(p j) c -> p (j c)", j=PACK))

@@ -87,14 +87,14 @@ def tile_picked_yqeq_pair_p_kernel(tc, x_words, x_scales, w1, w2, total, inv, of
                 out=w1_words[:, cols].bitcast(FP8X4), scales=w1_scales[:, cols], in_=w1_bf[u][:].rearrange("p t m j -> p (t m j)")
             )
 
-        for u, width in enumerate((H, P)):
-            pe_warm = ps.tile([P, width], F32, name="pe_warm%d" % u, tag="bank%d" % (BANKS - 1 - u))
+        for u in range(2):
+            pe_warm = ps.tile([P // 2, H], F32, name="pe_warm%d" % u, tag="bank%d" % (BANKS - 1 - u))
             nc.tensor.matmul_mx(
                 out=pe_warm[:],
-                lhsT=w1_words[:, :P].bitcast(FP8X4),
-                lhsT_scale=w1_scales[:, :P],
-                rhs=w1_words[:, :width].bitcast(FP8X4),
-                rhs_scale=w1_scales[:, :width],
+                lhsT=w1_words[:, : P // 2].bitcast(FP8X4),
+                lhsT_scale=w1_scales[:, : P // 2],
+                rhs=w1_words[:].bitcast(FP8X4),
+                rhs_scale=w1_scales[:],
                 start=True,
                 stop=True,
             )

@@ -24,7 +24,6 @@ BANKS = 8
 CHUNK = 128
 HALF = 256
 
-VECTOR_SHARE = 32
 W1_FIRST = 768
 PIECES = [(0, 128), (128, 256), (256, 384), (384, 448), (448, 512)]
 PAIR_RUNS = [(0, 256), (256, 384), (384, 512)]
@@ -75,10 +74,12 @@ def tile_picked_yqeq_pair_p_kernel(tc, x_words, x_scales, w1, w2, total, inv, of
         w1_view = w1_raw[:].rearrange("p j (m t) -> p m j t", t=PACK)
         w1_bf = [sb.tile([P, 2, P, PACK], BF16, name="w1_bf%d" % u, tag="w1_bf%d" % u, align_bytes=64) for u in range(2)]
         w1_dealt = [pair[:].rearrange("p t m j -> p m j t") for pair in w1_bf]
-        nc.vector.tensor_copy(w1_dealt[0], w1_view[:, :, :, 0:2])
-        nc.vector.tensor_copy(w1_dealt[1][:, :VECTOR_SHARE], w1_view[:, :VECTOR_SHARE, :, 2:4])
-        for lo, hi in ((VECTOR_SHARE, (VECTOR_SHARE + P) // 2), ((VECTOR_SHARE + P) // 2, P)):
-            nc.scalar.activation(w1_dealt[1][:, lo:hi], w1_view[:, lo:hi, :, 2:4], ACT.Copy)
+        early = (W1_FIRST - H) // PACK
+        for rows in (slice(0, 2), slice(2, PACK)):
+            for u in range(2):
+                nc.scalar.activation(w1_dealt[u][:, :early, rows], w1_view[:, :early, rows, 2 * u : 2 * u + 2], ACT.Copy)
+        for u in range(2):
+            nc.vector.tensor_copy(w1_dealt[u][:, early:], w1_view[:, early:, :, 2 * u : 2 * u + 2])
         w1_words = sb.tile([P, H], U32, name="w1_words", align_bytes=64)
         w1_scales = sb.tile([P, H], U8, name="w1_scales", align_bytes=64)
         for u in range(2):
@@ -123,9 +124,6 @@ def tile_picked_yqeq_pair_p_kernel(tc, x_words, x_scales, w1, w2, total, inv, of
         shifted = sb.tile([P, S], F32, name="shifted")
         h_ps, h_bf, y_ps = [], {}, {}
 
-        shared_scales = sb.tile([P, CHUNK], U8, name="shared_scales", align_bytes=64)
-        nc.vector.tensor_copy(shared_scales[:].bitcast(I32), x_scales_placed[:, S - CHUNK :].bitcast(I32))
-
         def first_product(c, operands):
             if c == len(h_ps):
                 h_ps.append(ps.tile([P, PACK, CHUNK], F32, name="h_ps%d" % c, tag="bank%d" % c))
@@ -138,7 +136,7 @@ def tile_picked_yqeq_pair_p_kernel(tc, x_words, x_scales, w1, w2, total, inv, of
                     lhsT=w1_words[:, cols].bitcast(FP8X4),
                     lhsT_scale=w1_scales[:, cols],
                     rhs=x_words_picked[u][:, start : start + CHUNK].bitcast(FP8X4),
-                    rhs_scale=shared_scales[:] if (c, t) == (chunks - 1, PACK - 1) else x_scales_placed[:, c * CHUNK : (c + 1) * CHUNK],
+                    rhs_scale=x_scales_placed[:, c * CHUNK : (c + 1) * CHUNK],
                     start=True,
                     stop=True,
                 )
@@ -152,7 +150,7 @@ def tile_picked_yqeq_pair_p_kernel(tc, x_words, x_scales, w1, w2, total, inv, of
         def second_product(c):
             lo, hi = PIECES[c]
             h_words = sb.tile([P, hi - lo], U32, name="h_words%d" % c, align_bytes=64)
-            h_scales = shared_scales[PACK:, :] if c == 0 else sb.tile([P, hi - lo], U8, name="h_scales%d" % c, align_bytes=64)[:]
+            h_scales = sb.tile([P, hi - lo], U8, name="h_scales%d" % c, align_bytes=64)[:]
             nc.vector.quantize_mx(out=h_words[:].bitcast(FP8X4), scales=h_scales, in_=h_bf[c][:].rearrange("p n t -> p (n t)"))
             y_ps[c] = ps.tile([P, hi - lo], F32, name="y_ps%d" % c, tag="bank%d" % [4, 2, 5, 6, 7][c])
             nc.tensor.matmul_mx(
@@ -183,15 +181,11 @@ def tile_picked_yqeq_pair_p_kernel(tc, x_words, x_scales, w1, w2, total, inv, of
                 ALU.add,
             )
 
-        for c in range(chunks - 1):
+        for c in range(chunks):
             first_product(c, range(PACK))
-        first_product(chunks - 1, range(PACK - 1))
-        silu(0)
-        second_product(0)
-        first_product(chunks - 1, [PACK - 1])
-        for c in range(1, len(PIECES)):
+        for c in range(len(PIECES)):
             silu(c)
-        for c in range(1, len(PIECES)):
+        for c in range(len(PIECES)):
             second_product(c)
         sum_y(0)
         shift_y(0)

@@ -26,7 +26,9 @@ HALF = 256
 
 W1_FIRST = 768
 PIECES = [(0, 128), (128, 256), (256, 384), (384, 448), (448, 512)]
-PAIR_RUNS = [(0, 256), (256, 384), (384, 512)]
+PAIR_RUNS = [(0, 128), (128, 256), (256, 384), (384, 512)]
+STORES = [(0, 256), (256, 384), (384, 512)]
+WORD_RUNS = [(0, 128), (128, 256), (256, 512)]
 
 
 def tile_picked_yqeq_pair_p_kernel(tc, x_words, x_scales, w1, w2, total, inv, offs, pa, pb, out):
@@ -60,9 +62,6 @@ def tile_picked_yqeq_pair_p_kernel(tc, x_words, x_scales, w1, w2, total, inv, of
         nc.sync.dma_start(pa_sb[:], pa)
         nc.sync.dma_start(pb_sb[:], pb)
 
-        def offs_half(u):
-            return offs_sb[:, u * HALF // LIST_ROWS : (u + 1) * HALF // LIST_ROWS]
-
         x_scales_picked = sb.tile([P, S], U8, name="x_scales_picked", align_bytes=64)
         nc.vector.tensor_copy(x_scales_picked[:], scales_all[:].indirect(offs_sb[:]))
         nc.vector.tensor_copy(x_scales_placed[:].bitcast(I32), x_scales_picked[:].bitcast(I32))
@@ -89,11 +88,11 @@ def tile_picked_yqeq_pair_p_kernel(tc, x_words, x_scales, w1, w2, total, inv, of
             )
 
         for u in range(2):
-            pe_warm = ps.tile([P // 2, H], F32, name="pe_warm%d" % u, tag="bank%d" % (BANKS - 1 - u))
+            pe_warm = ps.tile([P // 4, H], F32, name="pe_warm%d" % u, tag="bank%d" % (BANKS - 1 - u))
             nc.tensor.matmul_mx(
                 out=pe_warm[:],
-                lhsT=w1_words[:, : P // 2].bitcast(FP8X4),
-                lhsT_scale=w1_scales[:, : P // 2],
+                lhsT=w1_words[:, : P // 4].bitcast(FP8X4),
+                lhsT_scale=w1_scales[:, : P // 4],
                 rhs=w1_words[:].bitcast(FP8X4),
                 rhs_scale=w1_scales[:],
                 start=True,
@@ -106,11 +105,12 @@ def tile_picked_yqeq_pair_p_kernel(tc, x_words, x_scales, w1, w2, total, inv, of
         nc.sync.dma_start(total_sb, total)
         nc.sync.dma_start(inv_sb, inv)
 
-        x_words_picked = []
-        for u in range(2):
-            half = sb.tile([P, HALF], U32, name="x_words_picked%d" % u, align_bytes=64)
-            nc.vector.tensor_copy(half[:], words_all[:].indirect(offs_half(u)))
-            x_words_picked.append(half)
+        x_words_picked = {}
+        for lo, hi in WORD_RUNS:
+            picked = sb.tile([P, hi - lo], U32, name="x_words_picked%d" % lo, align_bytes=64)
+            nc.vector.tensor_copy(picked[:], words_all[:].indirect(offs_sb[:, lo // LIST_ROWS : hi // LIST_ROWS]))
+            for start in range(lo, hi, CHUNK):
+                x_words_picked[start] = picked[:, start - lo : start - lo + CHUNK]
 
         w2_bf = sb.tile([P, N, PACK], BF16, name="w2_bf", align_bytes=64)
         nc.vector.tensor_copy(w2_bf[:].rearrange("p (c i) j -> p c j i", i=4), w2_raw.rearrange("p (j c i) -> p c j i", j=PACK, i=4))
@@ -128,14 +128,13 @@ def tile_picked_yqeq_pair_p_kernel(tc, x_words, x_scales, w1, w2, total, inv, of
             if c == len(h_ps):
                 h_ps.append(ps.tile([P, PACK, CHUNK], F32, name="h_ps%d" % c, tag="bank%d" % c))
             bank = h_ps[c]
-            u, start = divmod(c * CHUNK, HALF)
             for t in operands:
                 cols = slice(t * P, (t + 1) * P)
                 nc.tensor.matmul_mx(
                     out=bank[:, t, :],
                     lhsT=w1_words[:, cols].bitcast(FP8X4),
                     lhsT_scale=w1_scales[:, cols],
-                    rhs=x_words_picked[u][:, start : start + CHUNK].bitcast(FP8X4),
+                    rhs=x_words_picked[c * CHUNK].bitcast(FP8X4),
                     rhs_scale=x_scales_placed[:, c * CHUNK : (c + 1) * CHUNK],
                     start=True,
                     stop=True,
@@ -198,17 +197,26 @@ def tile_picked_yqeq_pair_p_kernel(tc, x_words, x_scales, w1, w2, total, inv, of
         centre(PIECES[1][0], PIECES[-2][1])
         centre(*PIECES[-1])
 
-        left = []
-        for u in range(2):
-            factor = sb.tile([P, HALF], F32, name="left%d" % u)
-            entries = pa_sb[:, u * HALF // LIST_ROWS : (u + 1) * HALF // LIST_ROWS]
-            nc.vector.tensor_tensor(factor[:], ch[:].indirect(entries), inv_sb[:, u * HALF : (u + 1) * HALF], ALU.mult)
-            left.append(factor)
-        for lo, hi in PAIR_RUNS:
-            u, start = divmod(lo, HALF)
+        first, second = {}, {}
+        res = sb.tile([P, U], F32, name="res", align_bytes=64)
+
+        def fetch(lo, hi):
+            cols = slice(lo // LIST_ROWS, hi // LIST_ROWS)
+            first[lo] = sb.tile([P, hi - lo], F32, name="first%d" % lo)
+            second[lo] = sb.tile([P, hi - lo], F32, name="second%d" % lo)
+            nc.scalar.activation(first[lo][:], ch[:].indirect(pa_sb[:, cols]), ACT.Copy)
+            nc.vector.tensor_tensor(second[lo][:], ch[:].indirect(pb_sb[:, cols]), inv_sb[:, lo:hi], ALU.mult)
+
+        def finish(lo, hi):
             prod = sb.tile([P, hi - lo], F32, name="prod%d" % lo)
-            entries = pb_sb[:, lo // LIST_ROWS : hi // LIST_ROWS]
-            nc.vector.tensor_tensor(prod[:], ch[:].indirect(entries), left[u][:, start : start + hi - lo], ALU.mult)
-            res = sb.tile([P, hi - lo], F32, name="res%d" % lo)
-            nc.scalar.activation(res[:], prod[:], ACT.Tanh)
-            nc.sync.dma_start(out[:, lo:hi], res[:])
+            nc.vector.tensor_tensor(prod[:], first[lo][:], second[lo][:], ALU.mult)
+            nc.scalar.activation(res[:, lo:hi], prod[:], ACT.Tanh)
+            for start, stop in STORES:
+                if stop == hi:
+                    nc.sync.dma_start(out[:, start:stop], res[:, start:stop])
+
+        fetch(*PAIR_RUNS[0])
+        for run, following in zip(PAIR_RUNS, PAIR_RUNS[1:]):
+            fetch(*following)
+            finish(*run)
+        finish(*PAIR_RUNS[-1])

@@ -27,6 +27,7 @@ HALF = 256
 W1_FIRST = 768
 PIECES = [(0, 128), (128, 256), (256, 384), (384, 448), (448, 512)]
 PAIR_RUNS = [(0, 128), (128, 256), (256, 384), (384, 512)]
+LAG = 2
 STORES = [(0, 256), (256, 384), (384, 512)]
 WORD_RUNS = [(0, 128), (128, 256), (256, 512)]
 
@@ -215,8 +216,8 @@ def tile_picked_yqeq_pair_p_kernel(tc, x_words, x_scales, w1, w2, total, inv, of
                 if stop == hi:
                     nc.sync.dma_start(out[:, start:stop], res[:, start:stop])
 
-        fetch(*PAIR_RUNS[0])
-        for run, following in zip(PAIR_RUNS, PAIR_RUNS[1:]):
-            fetch(*following)
-            finish(*run)
-        finish(*PAIR_RUNS[-1])
+        for step in range(len(PAIR_RUNS) + LAG):
+            if step < len(PAIR_RUNS):
+                fetch(*PAIR_RUNS[step])
+            if step >= LAG:
+                finish(*PAIR_RUNS[step - LAG])

@@ -60,8 +60,6 @@ def tile_picked_yqeq_pair_p_kernel(tc, x_words, x_scales, w1, w2, total, inv, of
         nc.sync.dma_start(scales_all[0:P:BLOCK_ROWS, :].bitcast(I32), x_scales[0].bitcast(I32))
         nc.sync.dma_start(w1_flat[:, W1_FIRST:], w1_rows[:, W1_FIRST:])
         nc.sync.dma_start(words_all[:].bitcast(I32), x_words[0].rearrange("p n t -> p (n t)").bitcast(I32))
-        nc.sync.dma_start(pa_sb[:], pa)
-        nc.sync.dma_start(pb_sb[:], pb)
 
         x_scales_picked = sb.tile([P, S], U8, name="x_scales_picked", align_bytes=64)
         nc.vector.tensor_copy(x_scales_picked[:], scales_all[:].indirect(offs_sb[:]))
@@ -105,6 +103,8 @@ def tile_picked_yqeq_pair_p_kernel(tc, x_words, x_scales, w1, w2, total, inv, of
         nc.sync.dma_start(w2_raw, w2.rearrange("(p j) c -> p (j c)", j=PACK))
         nc.sync.dma_start(total_sb, total)
         nc.sync.dma_start(inv_sb, inv)
+        nc.sync.dma_start(pa_sb[:], pa)
+        nc.sync.dma_start(pb_sb[:], pb)
 
         x_words_picked = {}
         for lo, hi in WORD_RUNS:

@@ -28,6 +28,7 @@ W1_FIRST = 768
 PIECES = [(0, 128), (128, 256), (256, 384), (384, 448), (448, 512)]
 PAIR_RUNS = [(0, 128), (128, 256), (256, 384), (384, 512)]
 LAG = 2
+WARM_ROWS = 32
 STORES = [(0, 256), (256, 384), (384, 512)]
 WORD_RUNS = [(0, 128), (128, 256), (256, 512)]
 
@@ -86,14 +87,15 @@ def tile_picked_yqeq_pair_p_kernel(tc, x_words, x_scales, w1, w2, total, inv, of
                 out=w1_words[:, cols].bitcast(FP8X4), scales=w1_scales[:, cols], in_=w1_bf[u][:].rearrange("p t m j -> p (t m j)")
             )
 
-        for u in range(2):
-            pe_warm = ps.tile([P // 4, H], F32, name="pe_warm%d" % u, tag="bank%d" % (BANKS - 1 - u))
+        pe_warm = [ps.tile([WARM_ROWS, H], F32, name="pe_warm%d" % u, tag="bank%d" % (BANKS - 1 - u)) for u in range(2)]
+        windows = [(pe_warm[0][:, i * P : (i + 1) * P], slice(i % 2 * P, (i % 2 + 1) * P)) for i in range(H // P)]
+        for target, cols in windows + [(pe_warm[1][:], slice(0, H))]:
             nc.tensor.matmul_mx(
-                out=pe_warm[:],
-                lhsT=w1_words[:, : P // 4].bitcast(FP8X4),
-                lhsT_scale=w1_scales[:, : P // 4],
-                rhs=w1_words[:].bitcast(FP8X4),
-                rhs_scale=w1_scales[:],
+                out=target,
+                lhsT=w1_words[:, :WARM_ROWS].bitcast(FP8X4),
+                lhsT_scale=w1_scales[:, :WARM_ROWS],
+                rhs=w1_words[:, cols].bitcast(FP8X4),
+                rhs_scale=w1_scales[:, cols],
                 start=True,
                 stop=True,
             )

@@ -43,7 +43,7 @@ def tile_picked_yqeq_pair_p_kernel(tc, x_words, x_scales, w1, w2, total, inv, of
         pa_sb = sb.tile([P, U // LIST_ROWS], U16, name="pa_sb")
         pb_sb = sb.tile([P, U // LIST_ROWS], U16, name="pb_sb")
         words_all = sb.tile([P, T], U32, name="words_all", align_bytes=64)
-        scales_all = sb.tile([P, T], U8, name="scales_all", align_bytes=64)
+        scales_all = sb.tile([P, T], U8, name="scales_all", tag="scales_all", align_bytes=64)
         w1_raw = sb.tile([P, PACK, H], F32, name="w1_raw", tag="w1_raw", align_bytes=64)
         x_scales_placed = sb.tile([P, S], U8, name="x_scales_placed", align_bytes=64)
 
@@ -100,8 +100,10 @@ def tile_picked_yqeq_pair_p_kernel(tc, x_words, x_scales, w1, w2, total, inv, of
                 stop=True,
             )
 
-        late = sb.tile([P, 3 * S], F32, name="late", tag="w1_raw", align_bytes=64)
-        w2_raw, total_sb, inv_sb = late[:, :S], late[:, S : 2 * S], late[:, 2 * S :]
+        w2_tile = sb.tile([P, S], F32, name="w2_raw", tag="scales_all", align_bytes=64)
+        w2_raw = w2_tile[:]
+        late = sb.tile([P, 2 * S], F32, name="late", tag="w1_raw", align_bytes=64)
+        total_sb, inv_sb = late[:, :S], late[:, S:]
         nc.sync.dma_start(w2_raw, w2.rearrange("(p j) c -> p (j c)", j=PACK))
         nc.sync.dma_start(total_sb, total)
         nc.sync.dma_start(inv_sb, inv)

from contextlib import ExitStack

import concourse.mybir as mybir

K, T, S, D, H, N, U = 512, 2048, 512, 8, 512, 128, 512
FLOPS = 2 * K * H * S + 2 * H * N * S

F32 = mybir.dt.float32
BF16 = mybir.dt.bfloat16
I32 = mybir.dt.int32
U32 = mybir.dt.uint32
U16 = mybir.dt.uint16
U8 = mybir.dt.uint8
FP8X4 = mybir.dt.float8_e4m3fn_x4
ACT = mybir.ActivationFunctionType
ALU = mybir.AluOpType

P = 128
PACK = 4
QUADRANT = 32
BLOCK_ROWS = 8
LIST_ROWS = 16
BANKS = 8
CHUNK = 128
HALF = 256

W1_FIRST = 768
PIECES = [(0, 128), (128, 256), (256, 384), (384, 448), (448, 512)]
PAIR_RUNS = [(0, 128), (128, 256), (256, 384), (384, 512)]
LAG = 2
WARM_ROWS = 32
STORES = [(0, 256), (256, 384), (384, 512)]
WORD_RUNS = [(0, 128), (128, 256), (256, 512)]


def tile_picked_yqeq_pair_p_kernel(tc, x_words, x_scales, w1, w2, total, inv, offs, pa, pb, out):
    nc = tc.nc
    with ExitStack() as ctx:
        sb = ctx.enter_context(tc.tile_pool(name="sb", bufs=1))
        ps = ctx.enter_context(tc.psum_pool(name="ps", bufs=1))

        offs_sb = sb.tile([P, S // LIST_ROWS], U16, name="offs_sb")
        pa_sb = sb.tile([P, U // LIST_ROWS], U16, name="pa_sb")
        pb_sb = sb.tile([P, U // LIST_ROWS], U16, name="pb_sb")
        words_all = sb.tile([P, T], U32, name="words_all", align_bytes=64)
        scales_all = sb.tile([P, T], U8, name="scales_all", tag="scales_all", align_bytes=64)
        w1_raw = sb.tile([P, PACK, H], F32, name="w1_raw", tag="w1_raw", align_bytes=64)
        x_scales_placed = sb.tile([P, S], U8, name="x_scales_placed", align_bytes=64)

        nc.vector.memset(scales_all[:].bitcast(I32), 0)

        warm_in = sb.tile([P, 1], F32, name="warm_in")
        warm_out = sb.tile([P, 1], F32, name="warm_out")
        nc.gpsimd.memset(warm_in[:], 0.0)
        nc.scalar.activation(warm_out[:], warm_in[:], ACT.Silu)

        w1_rows = w1.rearrange("(p j) c -> p (j c)", j=PACK)
        w1_flat = w1_raw[:].rearrange("p j c -> p (j c)")
        nc.sync.dma_start(w1_flat[:, :W1_FIRST], w1_rows[:, :W1_FIRST])
        nc.sync.dma_start(offs_sb[:], offs)
        nc.sync.dma_start(scales_all[0:P:BLOCK_ROWS, :].bitcast(I32), x_scales[0].bitcast(I32))
        nc.sync.dma_start(w1_flat[:, W1_FIRST:], w1_rows[:, W1_FIRST:])
        nc.sync.dma_start(words_all[:].bitcast(I32), x_words[0].rearrange("p n t -> p (n t)").bitcast(I32))

        x_scales_picked = sb.tile([P, S], U8, name="x_scales_picked", align_bytes=64)
        nc.vector.tensor_copy(x_scales_picked[:], scales_all[:].indirect(offs_sb[:]))
        nc.vector.tensor_copy(x_scales_placed[:].bitcast(I32), x_scales_picked[:].bitcast(I32))
        for r in range(1, PACK):
            nc.sync.dma_start(
                x_scales_placed[r:P:QUADRANT, :].bitcast(I32), x_scales_picked[r * BLOCK_ROWS : P : QUADRANT, :].bitcast(I32)
            )

        w1_view = w1_raw[:].rearrange("p j (m t) -> p m j t", t=PACK)
        w1_bf = [sb.tile([P, 2, P, PACK], BF16, name="w1_bf%d" % u, tag="w1_bf%d" % u, align_bytes=64) for u in range(2)]
        w1_dealt = [pair[:].rearrange("p t m j -> p m j t") for pair in w1_bf]
        early = (W1_FIRST - H) // PACK
        for rows in (slice(0, 2), slice(2, PACK)):
            for u in range(2):
                nc.scalar.activation(w1_dealt[u][:, :early, rows], w1_view[:, :early, rows, 2 * u : 2 * u + 2], ACT.Copy)
        for u in range(2):
            nc.vector.tensor_copy(w1_dealt[u][:, early:], w1_view[:, early:, :, 2 * u : 2 * u + 2])
        w1_words = sb.tile([P, H], U32, name="w1_words", align_bytes=64)
        w1_scales = sb.tile([P, H], U8, name="w1_scales", align_bytes=64)
        for u in range(2):
            cols = slice(u * HALF, (u + 1) * HALF)
            nc.vector.quantize_mx(
                out=w1_words[:, cols].bitcast(FP8X4), scales=w1_scales[:, cols], in_=w1_bf[u][:].rearrange("p t m j -> p (t m j)")
            )

        pe_warm = [ps.tile([WARM_ROWS, H], F32, name="pe_warm%d" % u, tag="bank%d" % (BANKS - 1 - u)) for u in range(2)]
        windows = [(pe_warm[0][:, i * P : (i + 1) * P], slice(i % 2 * P, (i % 2 + 1) * P)) for i in range(H // P)]
        for target, cols in windows + [(pe_warm[1][:], slice(0, H))]:
            nc.tensor.matmul_mx(
                out=target,
                lhsT=w1_words[:, :WARM_ROWS].bitcast(FP8X4),
                lhsT_scale=w1_scales[:, :WARM_ROWS],
                rhs=w1_words[:, cols].bitcast(FP8X4),
                rhs_scale=w1_scales[:, cols],
                start=True,
                stop=True,
            )

        w2_tile = sb.tile([P, S], F32, name="w2_raw", tag="scales_all", align_bytes=64)
        w2_raw = w2_tile[:]
        late = sb.tile([P, 2 * S], F32, name="late", tag="w1_raw", align_bytes=64)
        total_sb, inv_sb = late[:, :S], late[:, S:]
        nc.sync.dma_start(w2_raw, w2.rearrange("(p j) c -> p (j c)", j=PACK))
        nc.sync.dma_start(total_sb, total)
        nc.sync.dma_start(inv_sb, inv)
        nc.sync.dma_start(pa_sb[:], pa)
        nc.sync.dma_start(pb_sb[:], pb)

        x_words_picked = {}
        for lo, hi in WORD_RUNS:
            picked = sb.tile([P, hi - lo], U32, name="x_words_picked%d" % lo, align_bytes=64)
            nc.vector.tensor_copy(picked[:], words_all[:].indirect(offs_sb[:, lo // LIST_ROWS : hi // LIST_ROWS]))
            for start in range(lo, hi, CHUNK):
                x_words_picked[start] = picked[:, start - lo : start - lo + CHUNK]

        w2_bf = sb.tile([P, N, PACK], BF16, name="w2_bf", align_bytes=64)
        nc.vector.tensor_copy(w2_bf[:].rearrange("p (c i) j -> p c j i", i=4), w2_raw.rearrange("p (j c i) -> p c j i", j=PACK, i=4))
        w2_words = sb.tile([P, N], U32, name="w2_words", align_bytes=64)
        w2_scales = sb.tile([P, N], U8, name="w2_scales", align_bytes=64)
        nc.vector.quantize_mx(out=w2_words[:].bitcast(FP8X4), scales=w2_scales[:], in_=w2_bf[:].rearrange("p n j -> p (n j)"))

        chunks = S // CHUNK
        ch = sb.tile([P, S], F32, name="ch", align_bytes=64)
        sums = sb.tile([P, S // D], F32, name="sums")
        shifted = sb.tile([P, S], F32, name="shifted")
        h_ps, h_bf, y_ps = [], {}, {}

        def first_product(c, operands):
            if c == len(h_ps):
                h_ps.append(ps.tile([P, PACK, CHUNK], F32, name="h_ps%d" % c, tag="bank%d" % c))
            bank = h_ps[c]
            for t in operands:
                cols = slice(t * P, (t + 1) * P)
                nc.tensor.matmul_mx(
                    out=bank[:, t, :],
                    lhsT=w1_words[:, cols].bitcast(FP8X4),
                    lhsT_scale=w1_scales[:, cols],
                    rhs=x_words_picked[c * CHUNK].bitcast(FP8X4),
                    rhs_scale=x_scales_placed[:, c * CHUNK : (c + 1) * CHUNK],
                    start=True,
                    stop=True,
                )

        def silu(c):
            lo, hi = PIECES[c]
            bank, start = divmod(lo, CHUNK)
            h_bf[c] = sb.tile([P, hi - lo, PACK], BF16, name="h_bf%d" % c, tag="h_bf%d" % c, align_bytes=64)
            nc.scalar.activation(h_bf[c][:], h_ps[bank][:, :, start : start + hi - lo].rearrange("p t n -> p n t"), ACT.Silu)

        def second_product(c):
            lo, hi = PIECES[c]
            h_words = sb.tile([P, hi - lo], U32, name="h_words%d" % c, align_bytes=64)
            h_scales = sb.tile([P, hi - lo], U8, name="h_scales%d" % c, align_bytes=64)[:]
            nc.vector.quantize_mx(out=h_words[:].bitcast(FP8X4), scales=h_scales, in_=h_bf[c][:].rearrange("p n t -> p (n t)"))
            y_ps[c] = ps.tile([P, hi - lo], F32, name="y_ps%d" % c, tag="bank%d" % [4, 2, 5, 6, 7][c])
            nc.tensor.matmul_mx(
                out=y_ps[c][:],
                lhsT=w2_words[:].bitcast(FP8X4),
                lhsT_scale=w2_scales[:],
                rhs=h_words[:].bitcast(FP8X4),
                rhs_scale=h_scales,
                start=True,
                stop=True,
            )

        def sum_y(c):
            lo, hi = PIECES[c]
            nc.vector.tensor_reduce(sums[:, lo // D : hi // D], y_ps[c][:].rearrange("p (v d) -> p v d", d=D), mybir.AxisListType.X, ALU.add)

        def shift_y(c):
            lo, hi = PIECES[c]
            nc.vector.tensor_tensor(shifted[:, lo:hi], y_ps[c][:], total_sb[:, lo:hi], ALU.add)

        def centre(lo, hi):
            nc.vector.scalar_tensor_tensor(
                ch[:, lo:hi].rearrange("p (v d) -> p v d", d=D),
                sums[:, lo // D : hi // D].unsqueeze(2).to_broadcast([P, (hi - lo) // D, D]),
                -1.0 / D,
                shifted[:, lo:hi].rearrange("p (v d) -> p v d", d=D),
                ALU.mult,
                ALU.add,
            )

        for c in range(chunks):
            first_product(c, range(PACK))
        for c in range(len(PIECES)):
            silu(c)
        for c in range(len(PIECES)):
            second_product(c)
        sum_y(0)
        shift_y(0)
        sum_y(1)
        centre(*PIECES[0])
        shift_y(1)
        for c in range(2, len(PIECES)):
            sum_y(c)
            shift_y(c)
        centre(PIECES[1][0], PIECES[-2][1])
        centre(*PIECES[-1])

        first, second = {}, {}
        res = sb.tile([P, U], F32, name="res", align_bytes=64)

        def fetch(lo, hi):
            cols = slice(lo // LIST_ROWS, hi // LIST_ROWS)
            first[lo] = sb.tile([P, hi - lo], F32, name="first%d" % lo)
            second[lo] = sb.tile([P, hi - lo], F32, name="second%d" % lo)
            nc.scalar.activation(first[lo][:], ch[:].indirect(pa_sb[:, cols]), ACT.Copy)
            nc.vector.tensor_tensor(second[lo][:], ch[:].indirect(pb_sb[:, cols]), inv_sb[:, lo:hi], ALU.mult)

        def finish(lo, hi):
            prod = sb.tile([P, hi - lo], F32, name="prod%d" % lo)
            nc.vector.tensor_tensor(prod[:], first[lo][:], second[lo][:], ALU.mult)
            nc.scalar.activation(res[:, lo:hi], prod[:], ACT.Tanh)
            for start, stop in STORES:
                if stop == hi:
                    nc.sync.dma_start(out[:, start:stop], res[:, start:stop])

        for step in range(len(PAIR_RUNS) + LAG):
            if step < len(PAIR_RUNS):
                fetch(*PAIR_RUNS[step])
            if step >= LAG:
                finish(*PAIR_RUNS[step - LAG])
